import numpy as np
import ml_dtypes


def mxq(x, axis, fmt="e4m3"):
    dtype, down = {"e4m3": (ml_dtypes.float8_e4m3fn, 7), "e5m2": (ml_dtypes.float8_e5m2, 14)}[fmt]
    v = np.moveaxis(np.asarray(x, np.float32).astype(ml_dtypes.bfloat16).astype(np.float64), axis, -1)
    blocks = v.reshape(v.shape[:-1] + (-1, 32))
    amax = np.abs(blocks).max(-1, keepdims=True)
    byte = np.maximum(np.where(amax > 0, np.frexp(amax)[1] - 1 + 127, 0) - down, 1)
    scale = np.exp2(byte - 127.0)
    codes = (blocks / scale).astype(np.float32).astype(dtype).astype(np.float64)
    return np.moveaxis((codes * scale).reshape(v.shape), -1, axis)


WIDE = False


def mx_kscale(k):
    if not WIDE:
        return np.ones(k)
    levels = np.array([24, -24, 12, -12, 0])
    if k % 512:
        return np.exp2(np.random.permutation(np.resize(levels, k // 32))).repeat(32)
    a = np.empty((k // 512, 16))
    for p in range(k // 512):
        a[p, :8] = np.random.permutation(np.resize(levels, 8))
        for g in range(8):
            far = levels[np.abs(levels - a[p, g]) >= 10]
            a[p, g + 8] = far[np.random.randint(len(far))]
    return np.exp2(a.ravel()).repeat(32)


def f64(x):
    return np.asarray(x).astype(np.float64)


def striped(idx):
    return np.tile(idx.reshape(-1, 16).T, (8, 1)).astype(np.uint16)


def unstriped(offs):
    return offs[:16].T.reshape(-1).astype(np.int64)


E2M1 = np.array([0.0, 0.5, 1.0, 1.5, 2.0, 3.0, 4.0, 6.0, -0.0, -0.5, -1.0, -1.5, -2.0, -3.0, -4.0, -6.0])


def pack_weight(w, fmt):
    k, n = w.shape
    w = f64(np.asarray(w, np.float32).astype(ml_dtypes.bfloat16)).reshape(k // 32, 32, n)
    amax = np.abs(w).max(1)
    if fmt == "e4m3":
        byte = np.frexp(amax)[1] - 1 + 127 - 7
    else:
        mant, ex = np.frexp(amax / 6.0)
        byte = np.where(mant > 0.5, ex, ex - 1) + 127
    byte = np.clip(np.where(amax > 0, byte, 1), 1, 254)
    scaled = (w * np.exp2(127.0 - byte)[:, None, :]).reshape(k, n).astype(np.float32)
    by_word = np.ascontiguousarray(scaled.reshape(k // 512, 128, 4, n).transpose(0, 1, 3, 2))
    if fmt == "e4m3":
        words = by_word.astype(ml_dtypes.float8_e4m3fn).view(np.uint8)
    else:
        c = by_word.astype(ml_dtypes.float4_e2m1fn).view(np.uint8) & 0xF
        words = (c[..., 0::2] | (c[..., 1::2] << 4)).reshape(k // 512, 128, 2 * n)
    return np.ascontiguousarray(words), np.ascontiguousarray(byte.astype(np.uint8).reshape(k // 512, 16, n))


def unpack_weight(words, scales, fmt):
    g, _, n = scales.shape
    words = np.ascontiguousarray(words).reshape(g, 128, n, -1)
    if fmt == "e4m3":
        vals = words.view(ml_dtypes.float8_e4m3fn).astype(np.float64)
    else:
        nib = np.empty((g, 128, n, 4), np.uint8)
        nib[..., 0::2] = words & 0xF
        nib[..., 1::2] = words >> 4
        vals = E2M1[nib]
    vals = vals * np.repeat(np.exp2(scales.astype(np.float64) - 127.0), 8, axis=1)[..., None]
    return vals.transpose(0, 1, 3, 2).reshape(g * 512, n)


def pack_table4(v):
    words, scales = pack_weight(v, "e2m1")
    g, t = words.shape[0] // 2, v.shape[1]
    return np.ascontiguousarray(words.reshape(g, 2, 128, t, 2).transpose(0, 2, 3, 1, 4).reshape(g, 128, t, 4)), scales


def unpack_table4(words, scales):
    g, _, t, _ = words.shape
    return unpack_weight(words.reshape(g, 128, t, 2, 2).transpose(0, 3, 1, 2, 4).reshape(2 * g, 128, 2 * t), scales, "e2m1")


K, L, R, N, T, J = 1024, 512, 512, 256, 4096, 1024


def setup_inputs():
    n = np.random.standard_normal
    s = mx_kscale(K)[:, None]
    s2 = mx_kscale(L)[:, None]
    u = mx_kscale(R)[:, None]
    p_tab = pack_table4(n((K, T)) * s)
    p_tab2 = pack_weight(n((L, T)) * s2, "e4m3")
    p_wer = pack_weight(n((K, R)) / np.sqrt(K) / s * u.T, "e4m3")
    p_wei = pack_weight(n((K, R)) / np.sqrt(K) / s * u.T, "e4m3")
    p_wrr = pack_weight(n((L, R)) / np.sqrt(L) / s2, "e2m1")
    p_wri = pack_weight(n((L, R)) / np.sqrt(L) / s2, "e2m1")
    return {
        "tab_words": p_tab[0],
        "tab_scales": p_tab[1],
        "tab2_words": p_tab2[0],
        "tab2_scales": p_tab2[1],
        "wer_words": p_wer[0],
        "wer_scales": p_wer[1],
        "wei_words": p_wei[0],
        "wei_scales": p_wei[1],
        "wrr_words": p_wrr[0],
        "wrr_scales": p_wrr[1],
        "wri_words": p_wri[0],
        "wri_scales": p_wri[1],
        "nr": (n((R, N)) / np.sqrt(R) / u).astype(np.float32),
        "ni": (n((R, N)) / np.sqrt(R) / u).astype(np.float32),
        "b": (0.3 * n(N)).astype(np.float32),
        "offs": striped(np.random.permutation(T)[:J]),
        "offs2": striped(np.random.permutation(T)[:J]),
    }


def reference(tab_words, tab_scales, tab2_words, tab2_scales, wer_words, wer_scales, wei_words, wei_scales, wrr_words, wrr_scales, wri_words, wri_scales, nr, ni, b, offs, offs2):
    idx = unstriped(offs)
    idx2 = unstriped(offs2)
    tab_ = unpack_table4(tab_words, tab_scales)[:, idx]
    tab2_ = unpack_weight(tab2_words, tab2_scales, "e4m3")[:, idx2]
    wer_ = unpack_weight(wer_words, wer_scales, "e4m3")
    aer = wer_.T @ tab_
    wei_ = unpack_weight(wei_words, wei_scales, "e4m3")
    aei = wei_.T @ tab_
    wrr_ = unpack_weight(wrr_words, wrr_scales, "e2m1")
    arr = wrr_.T @ tab2_
    wri_ = unpack_weight(wri_words, wri_scales, "e2m1")
    ari = wri_.T @ tab2_
    hr = aer * arr - aei * ari
    hi = aer * ari + aei * arr
    hr_ = mxq(hr, 0, "e4m3")
    hi_ = mxq(hi, 0, "e4m3")
    nr_ = mxq(f64(nr), 0, "e4m3")
    ni_ = mxq(f64(ni), 0, "e4m3")
    y = nr_.T @ hr_ + ni_.T @ hi_
    return y + f64(b)[:, None]

@@ -1,0 +1,241 @@
+from contextlib import ExitStack
+
+import concourse.mybir as mybir
+
+K, L, R, N, T, J = 1024, 512, 512, 256, 4096, 1024
+FLOPS = 2 * J * (2 * K * R + 2 * L * R + 2 * R * N)
+
+F32 = mybir.dt.float32
+BF16 = mybir.dt.bfloat16
+I32 = mybir.dt.int32
+U32 = mybir.dt.uint32
+U16 = mybir.dt.uint16
+U8 = mybir.dt.uint8
+FP8X4 = mybir.dt.float8_e4m3fn_x4
+FP4X4 = mybir.dt.float4_e2m1fn_x4
+MULT = mybir.AluOpType.mult
+ADD = mybir.AluOpType.add
+COPY = mybir.ActivationFunctionType.Copy
+IDENTITY = mybir.ActivationFunctionType.Identity
+
+P = 128
+PACK = 4
+JT = 128
+TILES = J // JT
+HALF = J // 2
+TILES_PER_HALF = HALF // JT
+ROWS = 32
+TAB_AT, WER_AT, WEI_AT, WR_AT, TAB2_AT = 0, J, J + R, J + 2 * R, J + 3 * R
+ODD_WIDTH, EVEN_WIDTH = TAB2_AT, TAB2_AT + J
+QUANT_LAG = 2
+AHEAD = 3
+
+
+def tile_list_ckg_bias_kernel(
+    tc, tab_words, tab_scales, tab2_words, tab2_scales, wer_words, wer_scales, wei_words, wei_scales,
+    wrr_words, wrr_scales, wri_words, wri_scales, nr, ni, b, offs, offs2, out,
+):
+    nc = tc.nc
+    with ExitStack() as ctx:
+        keep = ctx.enter_context(tc.tile_pool(name="keep", bufs=1))
+        raw = ctx.enter_context(tc.tile_pool(name="raw", bufs=1))
+        work = ctx.enter_context(tc.tile_pool(name="work", bufs=3))
+        psum = ctx.enter_context(tc.psum_pool(name="psum", bufs=2))
+
+        idx = keep.tile([P, J // 16], U16, name="idx")
+        idx2 = keep.tile([P, J // 16], U16, name="idx2")
+        tab_s = keep.tile([P, T // 4], I32, name="tab_s", align_bytes=64)
+        tab2_s = keep.tile([P, T // 4], I32, name="tab2_s", align_bytes=64)
+        tab_w = keep.tile([P, T], I32, name="tab_w", align_bytes=64)
+        tab2_w = keep.tile([P, T], I32, name="tab2_w", align_bytes=64)
+        w_s_raw = keep.tile([ROWS, 3, R // 4], I32, name="w_s_raw", align_bytes=64)
+        staged = keep.tile([ROWS, EVEN_WIDTH // 4], I32, name="staged", align_bytes=64)
+        even = keep.tile([P, EVEN_WIDTH // 4], I32, name="even", align_bytes=64)
+        odd = keep.tile([P, ODD_WIDTH // 4], I32, name="odd", align_bytes=64)
+        wer_raw = raw.tile([P, 2, R], I32, name="wer_raw", tag="raw_re")
+        wei_raw = raw.tile([P, 2, R], I32, name="wei_raw", tag="raw_im")
+        wr_raw = keep.tile([P, 2, R // 2], I32, name="wr_raw")
+        bias_raw = keep.tile([P, 2], F32, name="bias_raw")
+        bias = keep.tile([P, 2], F32, name="bias")
+
+        for window in (tab_s, tab2_s):
+            nc.vector.memset(window[32:64, :], 0)
+            nc.vector.memset(window[64:128, :], 0)
+        nc.vector.memset(odd[:], 0)
+        nc.vector.memset(even[:], 0)
+
+        nc.sync.dma_start(idx[:], offs)
+        nc.sync.dma_start(out=tab_s[0:ROWS, :], in_=tab_scales.rearrange("a q t -> q a t").bitcast(I32))
+        nc.gpsimd.dma_start(
+            out=tab2_s[0:ROWS, :], in_=tab2_scales[0].bitcast(I32).unsqueeze(1).to_broadcast([16, 2, T // 4])
+        )
+        nc.gpsimd.dma_start(out=bias_raw[:], in_=b.rearrange("(p h) -> p h", h=2))
+        nc.sync.dma_start(out=w_s_raw[:, 0, :], in_=wer_scales.rearrange("a q r -> q a r").bitcast(I32))
+        nc.sync.dma_start(out=w_s_raw[:, 1, :], in_=wei_scales.rearrange("a q r -> q a r").bitcast(I32))
+        nc.sync.dma_start(out=w_s_raw[0:ROWS:2, 2, :], in_=wrr_scales[0].bitcast(I32))
+        nc.sync.dma_start(out=w_s_raw[1:ROWS:2, 2, :], in_=wri_scales[0].bitcast(I32))
+        nc.sync.dma_start(out=wer_raw[:], in_=wer_words.rearrange("a p r i -> p a (r i)").bitcast(I32))
+        nc.sync.dma_start(out=wei_raw[:], in_=wei_words.rearrange("a p r i -> p a (r i)").bitcast(I32))
+        nc.sync.dma_start(idx2[:], offs2)
+        nc.sync.dma_start(out=wr_raw[:, 0, :], in_=wrr_words[0].bitcast(I32))
+        nc.sync.dma_start(out=wr_raw[:, 1, :], in_=wri_words[0].bitcast(I32))
+        nc.sync.dma_start(out=tab_w[:], in_=tab_words[0].rearrange("p t i -> p (t i)").bitcast(I32))
+        nc.sync.dma_start(out=tab2_w[:], in_=tab2_words[0].rearrange("p t i -> p (t i)").bitcast(I32))
+        nc.scalar.activation(out=bias[:], in_=bias_raw[:], func=IDENTITY)
+
+        got_s = keep.tile([P, J], U8, name="got_s", align_bytes=64)
+        got2_s = keep.tile([P, J], U8, name="got2_s", align_bytes=64)
+        nc.vector.tensor_copy(got_s[:], tab_s[:].bitcast(U8).indirect(idx[:]))
+        nc.vector.tensor_copy(out=staged[:, TAB_AT // 4 : WER_AT // 4], in_=got_s[0:ROWS, :].bitcast(I32))
+        nc.vector.tensor_copy(
+            out=staged[:, WER_AT // 4 : TAB2_AT // 4].rearrange("p (m t g w) -> p m t g w", m=3, t=PACK, w=2),
+            in_=w_s_raw[:].rearrange("p m (g t w) -> p m t g w", t=PACK, w=2),
+        )
+        for quad in range(4):
+            queue = nc.gpsimd if quad == 0 else nc.scalar
+            queue.dma_start(
+                out=odd[32 * quad : 32 * quad + 4, :],
+                in_=staged[8 * quad + 1 : 8 * quad + 8 : 2, 0 : ODD_WIDTH // 4],
+            )
+        nc.vector.tensor_copy(got2_s[:], tab2_s[:].bitcast(U8).indirect(idx2[:]))
+        nc.vector.tensor_copy(out=staged[:, TAB2_AT // 4 :], in_=got2_s[0:ROWS, :].bitcast(I32))
+        for quad in range(4):
+            nc.scalar.dma_start(out=even[32 * quad : 32 * quad + 4, :], in_=staged[8 * quad : 8 * quad + 8 : 2, :])
+        planes = (even[:].bitcast(U8), odd[:].bitcast(U8))
+
+        we = keep.tile([P, 2, 2, R], I32, name="we", align_bytes=64)
+        wr = keep.tile([P, 2, R // 2], I32, name="wr", align_bytes=64)
+        for part, src in enumerate((wer_raw, wei_raw)):
+            nc.vector.tensor_copy(
+                out=we[:, part, :, :].rearrange("p a (t g q) -> p a t g q", t=PACK, q=8),
+                in_=src[:].rearrange("p a (g t q) -> p a t g q", t=PACK, q=8),
+            )
+        nc.vector.tensor_copy(
+            out=wr[:].rearrange("p m (t g w) -> p m t g w", t=PACK, w=4),
+            in_=wr_raw[:].rearrange("p m (g t w) -> p m t g w", t=PACK, w=4),
+        )
+
+        n_raw = []
+        for mat, tag in ((nr, "raw_re"), (ni, "raw_im")):
+            rows = raw.tile([P, PACK, N], F32, name="n_" + tag, tag=tag)
+            for t in range(PACK):
+                nc.sync.dma_start(out=rows[:, t, :], in_=mat.rearrange("(g t q) n -> t g q n", t=PACK, q=8)[t])
+            n_raw.append(rows)
+
+        got_w = keep.tile([P, J], U32, name="got_w", align_bytes=64)
+        got2_w = keep.tile([P, J], U32, name="got2_w", align_bytes=64)
+        parted = keep.tile([P, 2, 2, 2 * HALF], U8, name="parted", align_bytes=64)
+        for half in range(2):
+            cols = slice(half * HALF, (half + 1) * HALF)
+            entries = slice(half * HALF // 16, (half + 1) * HALF // 16)
+            nc.vector.tensor_copy(got_w[:, cols], tab_w[:].bitcast(U32).indirect(idx[:, entries]))
+            nc.vector.tensor_copy(
+                out=parted[:, half, :, :].bitcast(U16),
+                in_=got_w[:, cols].bitcast(U16).rearrange("p (j d) -> p d j", d=2),
+            )
+        for half in range(2):
+            cols = slice(half * HALF, (half + 1) * HALF)
+            entries = slice(half * HALF // 16, (half + 1) * HALF // 16)
+            nc.vector.tensor_copy(got2_w[:, cols], tab2_w[:].bitcast(U32).indirect(idx2[:, entries]))
+
+        def entity(i):
+            half, at = divmod(i * JT, HALF)
+            ent = keep.tile([P, 3, JT, PACK], F32, name="ent%d" % i)
+            for part, w_at in enumerate((WER_AT, WEI_AT)):
+                acc = psum.tile([P, PACK, JT], F32, name="acc_e", tag="acc_e", bufs=3)
+                for t in range(PACK):
+                    for a in range(2):
+                        nc.tensor.matmul_mx(
+                            out=acc[:, t, :],
+                            lhsT=we[:, part, a, t * P : (t + 1) * P].bitcast(FP8X4),
+                            lhsT_scale=planes[a][:, w_at + t * P : w_at + (t + 1) * P],
+                            rhs=parted[:, half, a, 2 * at : 2 * (at + JT)].bitcast(FP4X4),
+                            rhs_scale=planes[a][:, TAB_AT + i * JT : TAB_AT + (i + 1) * JT],
+                            start=(a == 0),
+                            stop=(a == 1),
+                        )
+                by_j = acc[:].rearrange("p t j -> p j t")
+                nc.scalar.copy(out=ent[:, 1 + part, :, :], in_=by_j)
+                if part == 1:
+                    nc.scalar.activation(out=ent[:, 0, :, :], in_=by_j, func=COPY, scale=-1.0)
+            return ent
+
+        def products(i, ent):
+            prods = []
+            for part, first in ((0, 1), (1, 0)):
+                acc = psum.tile([P, PACK, JT], F32, name="acc_r", tag="acc_r", bufs=3)
+                for t in range(PACK):
+                    nc.tensor.matmul_mx(
+                        out=acc[:, t, :],
+                        lhsT=wr[:, part, t * P // 2 : (t + 1) * P // 2].bitcast(FP4X4),
+                        lhsT_scale=planes[part][:, WR_AT + t * P : WR_AT + (t + 1) * P],
+                        rhs=got2_w[:, i * JT : (i + 1) * JT].bitcast(FP8X4),
+                        rhs_scale=planes[0][:, TAB2_AT + i * JT : TAB2_AT + (i + 1) * JT],
+                        start=True,
+                        stop=True,
+                    )
+                prod = work.tile([P, 2, JT, PACK], F32, name="prod%d" % part, tag="prod%d" % part)
+                nc.vector.tensor_tensor(
+                    out=prod[:],
+                    in0=acc[:].rearrange("p t j -> p j t").unsqueeze(1).to_broadcast([P, 2, JT, PACK]),
+                    in1=ent[:, first : first + 2, :, :],
+                    op=MULT,
+                )
+                prods.append(prod)
+            return prods
+
+        def complex_sum(adder, prods):
+            h = work.tile([P, 2 * JT * PACK], BF16, name="h", tag="h", align_bytes=64, bufs=4)
+            flat = [prod[:].rearrange("p m j t -> p (m j t)") for prod in prods]
+            adder.tensor_tensor(out=h[:], in0=flat[0], in1=flat[1], op=ADD)
+            return h
+
+        n_codes = keep.tile([P, 2, N], U32, name="n_codes", align_bytes=64)
+        n_scales = keep.tile([P, 2, N], U8, name="n_scales", align_bytes=64)
+
+        def candidates():
+            n_bf = keep.tile([P, 2, 2, P, PACK], BF16, name="n_bf", align_bytes=64)
+            for part in range(2):
+                nc.scalar.copy(out=n_bf[:, part, :, :, :], in_=n_raw[part][:].rearrange("p t (m h) -> p h m t", h=2))
+            nc.vector.quantize_mx(
+                out=n_codes[:].rearrange("p m n -> p (m n)").bitcast(FP8X4),
+                scales=n_scales[:].rearrange("p m n -> p (m n)"),
+                in_=n_bf[:].rearrange("p a h m t -> p (a h m t)"),
+            )
+
+        def scores(i, h):
+            codes = work.tile([P, 2 * JT], U32, name="codes", tag="codes", align_bytes=64)
+            scales = work.tile([P, 2 * JT], U8, name="scales", tag="scales", align_bytes=64)
+            nc.vector.quantize_mx(out=codes[:].bitcast(FP8X4), scales=scales[:], in_=h[:])
+            acc = psum.tile([P, 2, JT], F32, name="acc_y", tag="acc_y", bufs=2)
+            y = work.tile([P, 2, JT], F32, name="y", tag="y")
+            for nh in range(2):
+                for part in range(2):
+                    nc.tensor.matmul_mx(
+                        out=acc[:, nh, :],
+                        lhsT=n_codes[:, part, nh * P : (nh + 1) * P].bitcast(FP8X4),
+                        lhsT_scale=n_scales[:, part, nh * P : (nh + 1) * P],
+                        rhs=codes[:, part * JT : (part + 1) * JT].bitcast(FP8X4),
+                        rhs_scale=scales[:, part * JT : (part + 1) * JT],
+                        start=(part == 0),
+                        stop=(part == 1),
+                    )
+            for nh in range(2):
+                nc.scalar.activation(out=y[:, nh, :], in_=acc[:, nh, :], func=IDENTITY, bias=bias[:, nh : nh + 1])
+            nc.sync.dma_start(out=out.rearrange("(p h) j -> p h j", h=2)[:, :, i * JT : (i + 1) * JT], in_=y[:])
+
+        ents = [entity(i) for i in range(AHEAD)]
+        hs = []
+        last = TILES - 1
+        for i in range(TILES):
+            prods = products(i, ents[i])
+            if i < last:
+                hs.append(complex_sum(nc.gpsimd, prods))
+            if i + AHEAD < TILES:
+                ents.append(entity(i + AHEAD))
+            if i == QUANT_LAG - 1:
+                candidates()
+            if i >= QUANT_LAG:
+                scores(i - QUANT_LAG, hs[i - QUANT_LAG])
+        scores(last - 1, hs[last - 1])
+        scores(last, complex_sum(nc.vector, prods))

@@ -24,11 +24,11 @@ JT = 128
 TILES = J // JT
 HALF = J // 2
 TILES_PER_HALF = HALF // JT
-ROWS = 32
+ROW0 = 96
 TAB_AT, WER_AT, WEI_AT, WR_AT, TAB2_AT = 0, J, J + R, J + 2 * R, J + 3 * R
 ODD_WIDTH, EVEN_WIDTH = TAB2_AT, TAB2_AT + J
 QUANT_LAG = 2
-AHEAD = 3
+AHEAD = 2
 
 
 def tile_list_ckg_bias_kernel(
@@ -45,11 +45,10 @@ def tile_list_ckg_bias_kernel(
         idx = keep.tile([P, J // 16], U16, name="idx")
         idx2 = keep.tile([P, J // 16], U16, name="idx2")
         tab_s = keep.tile([P, T // 4], I32, name="tab_s", align_bytes=64)
-        tab2_s = keep.tile([P, T // 4], I32, name="tab2_s", align_bytes=64)
+        tab2_s = raw.tile([P, T // 4], I32, name="tab2_s", tag="tab2", align_bytes=64)
         tab_w = keep.tile([P, T], I32, name="tab_w", align_bytes=64)
-        tab2_w = keep.tile([P, T], I32, name="tab2_w", align_bytes=64)
-        w_s_raw = keep.tile([ROWS, 3, R // 4], I32, name="w_s_raw", align_bytes=64)
-        staged = keep.tile([ROWS, EVEN_WIDTH // 4], I32, name="staged", align_bytes=64)
+        w_s_raw = keep.tile([P, 3, R // 4], I32, name="w_s_raw", align_bytes=64)
+        staged = keep.tile([P, EVEN_WIDTH // 4], I32, name="staged", align_bytes=64)
         even = keep.tile([P, EVEN_WIDTH // 4], I32, name="even", align_bytes=64)
         odd = keep.tile([P, ODD_WIDTH // 4], I32, name="odd", align_bytes=64)
         wer_raw = raw.tile([P, 2, R], I32, name="wer_raw", tag="raw_re")
@@ -59,49 +58,50 @@ def tile_list_ckg_bias_kernel(
         bias = keep.tile([P, 2], F32, name="bias")
 
         for window in (tab_s, tab2_s):
-            nc.vector.memset(window[32:64, :], 0)
-            nc.vector.memset(window[64:128, :], 0)
+            nc.vector.memset(window[0:ROW0, :], 0)
         nc.vector.memset(odd[:], 0)
         nc.vector.memset(even[:], 0)
 
         nc.sync.dma_start(idx[:], offs)
-        nc.sync.dma_start(out=tab_s[0:ROWS, :], in_=tab_scales.rearrange("a q t -> q a t").bitcast(I32))
+        nc.sync.dma_start(out=tab_s[ROW0:, :], in_=tab_scales.rearrange("a q t -> q a t").bitcast(I32))
+        nc.sync.dma_start(idx2[:], offs2)
         nc.gpsimd.dma_start(
-            out=tab2_s[0:ROWS, :], in_=tab2_scales[0].bitcast(I32).unsqueeze(1).to_broadcast([16, 2, T // 4])
+            out=tab2_s[ROW0:, :], in_=tab2_scales[0].bitcast(I32).unsqueeze(1).to_broadcast([16, 2, T // 4])
         )
         nc.gpsimd.dma_start(out=bias_raw[:], in_=b.rearrange("(p h) -> p h", h=2))
-        nc.sync.dma_start(out=w_s_raw[:, 0, :], in_=wer_scales.rearrange("a q r -> q a r").bitcast(I32))
-        nc.sync.dma_start(out=w_s_raw[:, 1, :], in_=wei_scales.rearrange("a q r -> q a r").bitcast(I32))
-        nc.sync.dma_start(out=w_s_raw[0:ROWS:2, 2, :], in_=wrr_scales[0].bitcast(I32))
-        nc.sync.dma_start(out=w_s_raw[1:ROWS:2, 2, :], in_=wri_scales[0].bitcast(I32))
+        nc.sync.dma_start(out=w_s_raw[ROW0:, 0, :], in_=wer_scales.rearrange("a q r -> q a r").bitcast(I32))
+        nc.sync.dma_start(out=w_s_raw[ROW0:, 1, :], in_=wei_scales.rearrange("a q r -> q a r").bitcast(I32))
+        nc.sync.dma_start(out=w_s_raw[ROW0:P:2, 2, :], in_=wrr_scales[0].bitcast(I32))
+        nc.sync.dma_start(out=w_s_raw[ROW0 + 1 : P : 2, 2, :], in_=wri_scales[0].bitcast(I32))
+        nc.sync.dma_start(out=tab_w[:], in_=tab_words[0].rearrange("p t i -> p (t i)").bitcast(I32))
         nc.sync.dma_start(out=wer_raw[:], in_=wer_words.rearrange("a p r i -> p a (r i)").bitcast(I32))
         nc.sync.dma_start(out=wei_raw[:], in_=wei_words.rearrange("a p r i -> p a (r i)").bitcast(I32))
-        nc.sync.dma_start(idx2[:], offs2)
         nc.sync.dma_start(out=wr_raw[:, 0, :], in_=wrr_words[0].bitcast(I32))
         nc.sync.dma_start(out=wr_raw[:, 1, :], in_=wri_words[0].bitcast(I32))
-        nc.sync.dma_start(out=tab_w[:], in_=tab_words[0].rearrange("p t i -> p (t i)").bitcast(I32))
-        nc.sync.dma_start(out=tab2_w[:], in_=tab2_words[0].rearrange("p t i -> p (t i)").bitcast(I32))
         nc.scalar.activation(out=bias[:], in_=bias_raw[:], func=IDENTITY)
 
         got_s = keep.tile([P, J], U8, name="got_s", align_bytes=64)
         got2_s = keep.tile([P, J], U8, name="got2_s", align_bytes=64)
-        nc.vector.tensor_copy(got_s[:], tab_s[:].bitcast(U8).indirect(idx[:]))
-        nc.vector.tensor_copy(out=staged[:, TAB_AT // 4 : WER_AT // 4], in_=got_s[0:ROWS, :].bitcast(I32))
+        halves = [
+            (slice(half * HALF, (half + 1) * HALF), slice(half * HALF // 16, (half + 1) * HALF // 16))
+            for half in range(2)
+        ]
+        for cols, entries in halves:
+            nc.vector.tensor_copy(got_s[:, cols], tab_s[:].bitcast(U8).indirect(idx[:, entries]))
         nc.vector.tensor_copy(
-            out=staged[:, WER_AT // 4 : TAB2_AT // 4].rearrange("p (m t g w) -> p m t g w", m=3, t=PACK, w=2),
-            in_=w_s_raw[:].rearrange("p m (g t w) -> p m t g w", t=PACK, w=2),
+            out=staged[ROW0:, WER_AT // 4 : TAB2_AT // 4].rearrange("p (m t g w) -> p m t g w", m=3, t=PACK, w=2),
+            in_=w_s_raw[ROW0:, :, :].rearrange("p m (g t w) -> p m t g w", t=PACK, w=2),
         )
-        for quad in range(4):
-            queue = nc.gpsimd if quad == 0 else nc.scalar
-            queue.dma_start(
-                out=odd[32 * quad : 32 * quad + 4, :],
-                in_=staged[8 * quad + 1 : 8 * quad + 8 : 2, 0 : ODD_WIDTH // 4],
-            )
+        nc.vector.tensor_copy(out=staged[ROW0:, TAB_AT // 4 : WER_AT // 4], in_=got_s[ROW0:, :].bitcast(I32))
+        for r in range(4):
+            nc.scalar.dma_start(out=odd[r:P:32, :], in_=staged[ROW0 + 2 * r + 1 : P : 8, 0 : ODD_WIDTH // 4])
         nc.vector.tensor_copy(got2_s[:], tab2_s[:].bitcast(U8).indirect(idx2[:]))
-        nc.vector.tensor_copy(out=staged[:, TAB2_AT // 4 :], in_=got2_s[0:ROWS, :].bitcast(I32))
-        for quad in range(4):
-            nc.scalar.dma_start(out=even[32 * quad : 32 * quad + 4, :], in_=staged[8 * quad : 8 * quad + 8 : 2, :])
+        nc.vector.tensor_copy(out=staged[ROW0:, TAB2_AT // 4 :], in_=got2_s[ROW0:, :].bitcast(I32))
+        for r in range(4):
+            nc.scalar.dma_start(out=even[r:P:32, :], in_=staged[ROW0 + 2 * r : P : 8, :])
         planes = (even[:].bitcast(U8), odd[:].bitcast(U8))
+        tab2_w = raw.tile([P, T], I32, name="tab2_w", tag="tab2", align_bytes=64)
+        nc.sync.dma_start(out=tab2_w[:], in_=tab2_words[0].rearrange("p t i -> p (t i)").bitcast(I32))
 
         we = keep.tile([P, 2, 2, R], I32, name="we", align_bytes=64)
         wr = keep.tile([P, 2, R // 2], I32, name="wr", align_bytes=64)
@@ -125,24 +125,20 @@ def tile_list_ckg_bias_kernel(
         got_w = keep.tile([P, J], U32, name="got_w", align_bytes=64)
         got2_w = keep.tile([P, J], U32, name="got2_w", align_bytes=64)
         parted = keep.tile([P, 2, 2, 2 * HALF], U8, name="parted", align_bytes=64)
-        for half in range(2):
-            cols = slice(half * HALF, (half + 1) * HALF)
-            entries = slice(half * HALF // 16, (half + 1) * HALF // 16)
+        for half, (cols, entries) in enumerate(halves):
             nc.vector.tensor_copy(got_w[:, cols], tab_w[:].bitcast(U32).indirect(idx[:, entries]))
             nc.vector.tensor_copy(
                 out=parted[:, half, :, :].bitcast(U16),
                 in_=got_w[:, cols].bitcast(U16).rearrange("p (j d) -> p d j", d=2),
             )
-        for half in range(2):
-            cols = slice(half * HALF, (half + 1) * HALF)
-            entries = slice(half * HALF // 16, (half + 1) * HALF // 16)
+        for cols, entries in halves:
             nc.vector.tensor_copy(got2_w[:, cols], tab2_w[:].bitcast(U32).indirect(idx2[:, entries]))
 
         def entity(i):
             half, at = divmod(i * JT, HALF)
             ent = keep.tile([P, 3, JT, PACK], F32, name="ent%d" % i)
             for part, w_at in enumerate((WER_AT, WEI_AT)):
-                acc = psum.tile([P, PACK, JT], F32, name="acc_e", tag="acc_e", bufs=3)
+                acc = psum.tile([P, PACK, JT], F32, name="acc_e", tag="acc_e", bufs=2)
                 for t in range(PACK):
                     for a in range(2):
                         nc.tensor.matmul_mx(
@@ -160,10 +156,10 @@ def tile_list_ckg_bias_kernel(
                     nc.scalar.activation(out=ent[:, 0, :, :], in_=by_j, func=COPY, scale=-1.0)
             return ent
 
-        def products(i, ent):
-            prods = []
-            for part, first in ((0, 1), (1, 0)):
-                acc = psum.tile([P, PACK, JT], F32, name="acc_r", tag="acc_r", bufs=3)
+        def relation(i):
+            accs = []
+            for part in range(2):
+                acc = psum.tile([P, PACK, JT], F32, name="acc_r", tag="acc_r", bufs=4)
                 for t in range(PACK):
                     nc.tensor.matmul_mx(
                         out=acc[:, t, :],
@@ -174,11 +170,18 @@ def tile_list_ckg_bias_kernel(
                         start=True,
                         stop=True,
                     )
+                accs.append(acc)
+            return accs
+
+        def products(ent, accs):
+            prods = []
+            for part, first in ((0, 1), (1, 0)):
+                acc = accs[part]
                 prod = work.tile([P, 2, JT, PACK], F32, name="prod%d" % part, tag="prod%d" % part)
                 nc.vector.tensor_tensor(
                     out=prod[:],
-                    in0=acc[:].rearrange("p t j -> p j t").unsqueeze(1).to_broadcast([P, 2, JT, PACK]),
-                    in1=ent[:, first : first + 2, :, :],
+                    in0=ent[:, first : first + 2, :, :],
+                    in1=acc[:].rearrange("p t j -> p j t").unsqueeze(1).to_broadcast([P, 2, JT, PACK]),
                     op=MULT,
                 )
                 prods.append(prod)
@@ -193,10 +196,13 @@ def tile_list_ckg_bias_kernel(
         n_codes = keep.tile([P, 2, N], U32, name="n_codes", align_bytes=64)
         n_scales = keep.tile([P, 2, N], U8, name="n_scales", align_bytes=64)
 
-        def candidates():
-            n_bf = keep.tile([P, 2, 2, P, PACK], BF16, name="n_bf", align_bytes=64)
+        n_bf = keep.tile([P, 2, 2, P, PACK], BF16, name="n_bf", align_bytes=64)
+
+        def round_candidates():
             for part in range(2):
                 nc.scalar.copy(out=n_bf[:, part, :, :, :], in_=n_raw[part][:].rearrange("p t (m h) -> p h m t", h=2))
+
+        def quantise_candidates():
             nc.vector.quantize_mx(
                 out=n_codes[:].rearrange("p m n -> p (m n)").bitcast(FP8X4),
                 scales=n_scales[:].rearrange("p m n -> p (m n)"),
@@ -225,16 +231,21 @@ def tile_list_ckg_bias_kernel(
             nc.sync.dma_start(out=out.rearrange("(p h) j -> p h j", h=2)[:, :, i * JT : (i + 1) * JT], in_=y[:])
 
         ents = [entity(i) for i in range(AHEAD)]
+        rels = [relation(0)]
         hs = []
         last = TILES - 1
         for i in range(TILES):
-            prods = products(i, ents[i])
+            if i < last:
+                rels.append(relation(i + 1))
+            prods = products(ents[i], rels[i])
             if i < last:
                 hs.append(complex_sum(nc.gpsimd, prods))
             if i + AHEAD < TILES:
                 ents.append(entity(i + AHEAD))
             if i == QUANT_LAG - 1:
-                candidates()
+                round_candidates()
+            if i == QUANT_LAG:
+                quantise_candidates()
             if i >= QUANT_LAG:
                 scores(i - QUANT_LAG, hs[i - QUANT_LAG])
         scores(last - 1, hs[last - 1])

@@ -15,7 +15,6 @@ FP8X4 = mybir.dt.float8_e4m3fn_x4
 FP4X4 = mybir.dt.float4_e2m1fn_x4
 MULT = mybir.AluOpType.mult
 ADD = mybir.AluOpType.add
-COPY = mybir.ActivationFunctionType.Copy
 IDENTITY = mybir.ActivationFunctionType.Identity
 
 P = 128
@@ -24,7 +23,7 @@ JT = 128
 TILES = J // JT
 HALF = J // 2
 TILES_PER_HALF = HALF // JT
-ROW0 = 96
+ROW0, ROW1 = 96, 112
 TAB_AT, WER_AT, WEI_AT, WR_AT, TAB2_AT = 0, J, J + R, J + 2 * R, J + 3 * R
 ODD_WIDTH, EVEN_WIDTH = TAB2_AT, TAB2_AT + J
 QUANT_LAG = 2
@@ -45,43 +44,35 @@ def tile_list_ckg_bias_kernel(
         idx = keep.tile([P, J // 16], U16, name="idx")
         idx2 = keep.tile([P, J // 16], U16, name="idx2")
         tab_s = keep.tile([P, T // 4], I32, name="tab_s", align_bytes=64)
-        tab2_s = raw.tile([P, T // 4], I32, name="tab2_s", tag="tab2", align_bytes=64)
-        tab_w = keep.tile([P, T], I32, name="tab_w", align_bytes=64)
+        tab2_s = keep.tile([P, T // 4], I32, name="tab2_s", align_bytes=64)
+        tab_w = raw.tile([P, T], I32, name="tab_w", tag="then_candidates", align_bytes=64)
         w_s_raw = keep.tile([P, 3, R // 4], I32, name="w_s_raw", align_bytes=64)
         staged = keep.tile([P, EVEN_WIDTH // 4], I32, name="staged", align_bytes=64)
         even = keep.tile([P, EVEN_WIDTH // 4], I32, name="even", align_bytes=64)
         odd = keep.tile([P, ODD_WIDTH // 4], I32, name="odd", align_bytes=64)
-        wer_raw = raw.tile([P, 2, R], I32, name="wer_raw", tag="raw_re")
-        wei_raw = raw.tile([P, 2, R], I32, name="wei_raw", tag="raw_im")
-        wr_raw = keep.tile([P, 2, R // 2], I32, name="wr_raw")
         bias_raw = keep.tile([P, 2], F32, name="bias_raw")
         bias = keep.tile([P, 2], F32, name="bias")
 
-        for window in (tab_s, tab2_s):
-            nc.vector.memset(window[0:ROW0, :], 0)
-        nc.vector.memset(odd[:], 0)
-        nc.vector.memset(even[:], 0)
+        nc.vector.memset(tab_s[0:ROW0, :], 0)
+        nc.vector.memset(tab2_s[:], 0)
+        nc.gpsimd.memset(odd[:], 0)
+        nc.gpsimd.memset(even[:], 0)
 
         nc.sync.dma_start(idx[:], offs)
-        nc.sync.dma_start(out=tab_s[ROW0:, :], in_=tab_scales.rearrange("a q t -> q a t").bitcast(I32))
+        nc.sync.dma_start(out=tab_s[ROW0:, :], in_=tab_scales.rearrange("a q t -> (a q) t").bitcast(I32))
         nc.sync.dma_start(idx2[:], offs2)
-        nc.gpsimd.dma_start(
-            out=tab2_s[ROW0:, :], in_=tab2_scales[0].bitcast(I32).unsqueeze(1).to_broadcast([16, 2, T // 4])
-        )
+        nc.scalar.dma_start(out=w_s_raw[ROW0:, 0, :], in_=wer_scales.rearrange("a q r -> (a q) r").bitcast(I32))
+        nc.scalar.dma_start(out=w_s_raw[ROW0:, 1, :], in_=wei_scales.rearrange("a q r -> (a q) r").bitcast(I32))
+        nc.scalar.dma_start(out=w_s_raw[ROW0:ROW1, 2, :], in_=wrr_scales[0].bitcast(I32))
+        nc.scalar.dma_start(out=w_s_raw[ROW1:, 2, :], in_=wri_scales[0].bitcast(I32))
+        tab_rows = tab_words[0].rearrange("p t i -> p (t i)").bitcast(I32)
+        nc.sync.dma_start(out=tab_w[:, : T // 2], in_=tab_rows[:, : T // 2])
+        nc.sync.dma_start(out=tab2_s[ROW0:ROW1, :], in_=tab2_scales[0].bitcast(I32))
+        nc.sync.dma_start(out=tab_w[:, T // 2 :], in_=tab_rows[:, T // 2 :])
         nc.gpsimd.dma_start(out=bias_raw[:], in_=b.rearrange("(p h) -> p h", h=2))
-        nc.sync.dma_start(out=w_s_raw[ROW0:, 0, :], in_=wer_scales.rearrange("a q r -> q a r").bitcast(I32))
-        nc.sync.dma_start(out=w_s_raw[ROW0:, 1, :], in_=wei_scales.rearrange("a q r -> q a r").bitcast(I32))
-        nc.sync.dma_start(out=w_s_raw[ROW0:P:2, 2, :], in_=wrr_scales[0].bitcast(I32))
-        nc.sync.dma_start(out=w_s_raw[ROW0 + 1 : P : 2, 2, :], in_=wri_scales[0].bitcast(I32))
-        nc.sync.dma_start(out=tab_w[:], in_=tab_words[0].rearrange("p t i -> p (t i)").bitcast(I32))
-        nc.sync.dma_start(out=wer_raw[:], in_=wer_words.rearrange("a p r i -> p a (r i)").bitcast(I32))
-        nc.sync.dma_start(out=wei_raw[:], in_=wei_words.rearrange("a p r i -> p a (r i)").bitcast(I32))
-        nc.sync.dma_start(out=wr_raw[:, 0, :], in_=wrr_words[0].bitcast(I32))
-        nc.sync.dma_start(out=wr_raw[:, 1, :], in_=wri_words[0].bitcast(I32))
         nc.scalar.activation(out=bias[:], in_=bias_raw[:], func=IDENTITY)
 
-        got_s = keep.tile([P, J], U8, name="got_s", align_bytes=64)
-        got2_s = keep.tile([P, J], U8, name="got2_s", align_bytes=64)
+        got_s = raw.tile([P, J], U8, name="got_s", tag="then_we", align_bytes=64)
         halves = [
             (slice(half * HALF, (half + 1) * HALF), slice(half * HALF // 16, (half + 1) * HALF // 16))
             for half in range(2)
@@ -94,49 +85,68 @@ def tile_list_ckg_bias_kernel(
         )
         nc.vector.tensor_copy(out=staged[ROW0:, TAB_AT // 4 : WER_AT // 4], in_=got_s[ROW0:, :].bitcast(I32))
         for r in range(4):
-            nc.scalar.dma_start(out=odd[r:P:32, :], in_=staged[ROW0 + 2 * r + 1 : P : 8, 0 : ODD_WIDTH // 4])
-        nc.vector.tensor_copy(got2_s[:], tab2_s[:].bitcast(U8).indirect(idx2[:]))
-        nc.vector.tensor_copy(out=staged[ROW0:, TAB2_AT // 4 :], in_=got2_s[ROW0:, :].bitcast(I32))
+            nc.sync.dma_start(out=odd[r:P:32, :], in_=staged[ROW1 + r : P : 4, 0 : ODD_WIDTH // 4])
+        w_raw = raw.tile([P, 5, R], I32, name="w_raw", tag="then_we", align_bytes=64)
+        we_raw = w_raw[:, 0:4, :].rearrange("p (m a) r -> p m a r", a=2)
+        wr_raw = w_raw[:, 4, :].rearrange("p (m w) -> p m w", m=2)
+        for part, words in enumerate((wer_words, wei_words)):
+            nc.sync.dma_start(out=we_raw[:, part, :, :], in_=words.rearrange("a p r i -> p a (r i)").bitcast(I32))
+        for part, words in enumerate((wrr_words, wri_words)):
+            nc.sync.dma_start(out=wr_raw[:, part, :], in_=words[0].bitcast(I32))
+        got2_s = []
+        for (cols, entries), tag in zip(halves, ("then_got_w", "then_tab2")):
+            got = raw.tile([P, HALF], U8, name="got2_s", tag=tag, align_bytes=64)
+            nc.vector.tensor_copy(got[:], tab2_s[:].bitcast(U8).indirect(idx2[:, entries]))
+            got2_s.append(got)
+        for half, got in enumerate(got2_s):
+            at = (TAB2_AT + half * HALF) // 4
+            nc.vector.tensor_copy(out=staged[ROW0:, at : at + HALF // 4], in_=got[ROW0:, :].bitcast(I32))
         for r in range(4):
-            nc.scalar.dma_start(out=even[r:P:32, :], in_=staged[ROW0 + 2 * r : P : 8, :])
+            nc.sync.dma_start(out=even[r:P:32, :], in_=staged[ROW0 + r : ROW1 : 4, :])
         planes = (even[:].bitcast(U8), odd[:].bitcast(U8))
-        tab2_w = raw.tile([P, T], I32, name="tab2_w", tag="tab2", align_bytes=64)
+        tab2_w = raw.tile([P, T], I32, name="tab2_w", tag="then_tab2", align_bytes=64)
         nc.sync.dma_start(out=tab2_w[:], in_=tab2_words[0].rearrange("p t i -> p (t i)").bitcast(I32))
 
+        got_w = raw.tile([P, J], U32, name="got_w", tag="then_got_w", align_bytes=64)
+        got2_w = []
+        parted = keep.tile([P, 2, 2, 2 * HALF], U8, name="parted", align_bytes=64)
         we = keep.tile([P, 2, 2, R], I32, name="we", align_bytes=64)
         wr = keep.tile([P, 2, R // 2], I32, name="wr", align_bytes=64)
-        for part, src in enumerate((wer_raw, wei_raw)):
-            nc.vector.tensor_copy(
-                out=we[:, part, :, :].rearrange("p a (t g q) -> p a t g q", t=PACK, q=8),
-                in_=src[:].rearrange("p a (g t q) -> p a t g q", t=PACK, q=8),
-            )
-        nc.vector.tensor_copy(
-            out=wr[:].rearrange("p m (t g w) -> p m t g w", t=PACK, w=4),
-            in_=wr_raw[:].rearrange("p m (g t w) -> p m t g w", t=PACK, w=4),
-        )
 
-        n_raw = []
-        for mat, tag in ((nr, "raw_re"), (ni, "raw_im")):
-            rows = raw.tile([P, PACK, N], F32, name="n_" + tag, tag=tag)
-            for t in range(PACK):
-                nc.sync.dma_start(out=rows[:, t, :], in_=mat.rearrange("(g t q) n -> t g q n", t=PACK, q=8)[t])
-            n_raw.append(rows)
-
-        got_w = keep.tile([P, J], U32, name="got_w", align_bytes=64)
-        got2_w = keep.tile([P, J], U32, name="got2_w", align_bytes=64)
-        parted = keep.tile([P, 2, 2, 2 * HALF], U8, name="parted", align_bytes=64)
-        for half, (cols, entries) in enumerate(halves):
+        def entity_words(half):
+            cols, entries = halves[half]
             nc.vector.tensor_copy(got_w[:, cols], tab_w[:].bitcast(U32).indirect(idx[:, entries]))
             nc.vector.tensor_copy(
                 out=parted[:, half, :, :].bitcast(U16),
                 in_=got_w[:, cols].bitcast(U16).rearrange("p (j d) -> p d j", d=2),
             )
-        for cols, entries in halves:
-            nc.vector.tensor_copy(got2_w[:, cols], tab2_w[:].bitcast(U32).indirect(idx2[:, entries]))
+
+        def relation_words(half):
+            got = keep.tile([P, HALF], U32, name="got2_w%d" % half, align_bytes=64)
+            nc.vector.tensor_copy(got[:], tab2_w[:].bitcast(U32).indirect(idx2[:, halves[half][1]]))
+            got2_w.append(got)
+
+        entity_words(0)
+        for part in range(2):
+            nc.vector.tensor_copy(
+                out=we[:, part, :, :].rearrange("p a (t g q) -> p a t g q", t=PACK, q=8),
+                in_=we_raw[:, part, :, :].rearrange("p a (g t q) -> p a t g q", t=PACK, q=8),
+            )
+        nc.vector.tensor_copy(
+            out=wr[:].rearrange("p m (t g w) -> p m t g w", t=PACK, w=4),
+            in_=wr_raw.rearrange("p m (g t w) -> p m t g w", t=PACK, w=4),
+        )
+        entity_words(1)
+        n_raw = raw.tile([P, 2, PACK, N], F32, name="n_raw", tag="then_candidates", align_bytes=64)
+        for part, mat in enumerate((nr, ni)):
+            for t in range(PACK):
+                nc.sync.dma_start(out=n_raw[:, part, t, :], in_=mat.rearrange("(g t q) n -> t g q n", t=PACK, q=8)[t])
+        relation_words(0)
+        relation_words(1)
 
         def entity(i):
             half, at = divmod(i * JT, HALF)
-            ent = keep.tile([P, 3, JT, PACK], F32, name="ent%d" % i)
+            ent = work.tile([P, 2, JT, PACK], F32, name="ent", tag="ent", bufs=AHEAD)
             for part, w_at in enumerate((WER_AT, WEI_AT)):
                 acc = psum.tile([P, PACK, JT], F32, name="acc_e", tag="acc_e", bufs=2)
                 for t in range(PACK):
@@ -150,13 +160,11 @@ def tile_list_ckg_bias_kernel(
                             start=(a == 0),
                             stop=(a == 1),
                         )
-                by_j = acc[:].rearrange("p t j -> p j t")
-                nc.scalar.copy(out=ent[:, 1 + part, :, :], in_=by_j)
-                if part == 1:
-                    nc.scalar.activation(out=ent[:, 0, :, :], in_=by_j, func=COPY, scale=-1.0)
+                nc.scalar.copy(out=ent[:, part, :, :], in_=acc[:].rearrange("p t j -> p j t"))
             return ent
 
         def relation(i):
+            half, at = divmod(i * JT, HALF)
             accs = []
             for part in range(2):
                 acc = psum.tile([P, PACK, JT], F32, name="acc_r", tag="acc_r", bufs=4)
@@ -165,7 +173,7 @@ def tile_list_ckg_bias_kernel(
                         out=acc[:, t, :],
                         lhsT=wr[:, part, t * P // 2 : (t + 1) * P // 2].bitcast(FP4X4),
                         lhsT_scale=planes[part][:, WR_AT + t * P : WR_AT + (t + 1) * P],
-                        rhs=got2_w[:, i * JT : (i + 1) * JT].bitcast(FP8X4),
+                        rhs=got2_w[half][:, at : at + JT].bitcast(FP8X4),
                         rhs_scale=planes[0][:, TAB2_AT + i * JT : TAB2_AT + (i + 1) * JT],
                         start=True,
                         stop=True,
@@ -174,18 +182,17 @@ def tile_list_ckg_bias_kernel(
             return accs
 
         def products(ent, accs):
-            prods = []
-            for part, first in ((0, 1), (1, 0)):
-                acc = accs[part]
-                prod = work.tile([P, 2, JT, PACK], F32, name="prod%d" % part, tag="prod%d" % part)
-                nc.vector.tensor_tensor(
-                    out=prod[:],
-                    in0=ent[:, first : first + 2, :, :],
-                    in1=acc[:].rearrange("p t j -> p j t").unsqueeze(1).to_broadcast([P, 2, JT, PACK]),
-                    op=MULT,
-                )
-                prods.append(prod)
-            return prods
+            arr, ari = (acc[:].rearrange("p t j -> p j t") for acc in accs)
+            with_re = work.tile([P, 2, JT, PACK], F32, name="with_re", tag="with_re")
+            with_im = work.tile([P, 2, JT, PACK], F32, name="with_im", tag="with_im")
+            nc.vector.tensor_tensor(
+                out=with_re[:], in0=ent[:], in1=arr.unsqueeze(1).to_broadcast([P, 2, JT, PACK]), op=MULT
+            )
+            nc.vector.scalar_tensor_tensor(
+                out=with_im[:, 0, :, :], in0=ent[:, 1, :, :], scalar=-1.0, in1=ari, op0=MULT, op1=MULT
+            )
+            nc.vector.tensor_tensor(out=with_im[:, 1, :, :], in0=ent[:, 0, :, :], in1=ari, op=MULT)
+            return with_re, with_im
 
         def complex_sum(adder, prods):
             h = work.tile([P, 2 * JT * PACK], BF16, name="h", tag="h", align_bytes=64, bufs=4)
@@ -200,7 +207,7 @@ def tile_list_ckg_bias_kernel(
 
         def round_candidates():
             for part in range(2):
-                nc.scalar.copy(out=n_bf[:, part, :, :, :], in_=n_raw[part][:].rearrange("p t (m h) -> p h m t", h=2))
+                nc.scalar.copy(out=n_bf[:, part, :, :, :], in_=n_raw[:, part, :, :].rearrange("p t (m h) -> p h m t", h=2))
 
         def quantise_candidates():
             nc.vector.quantize_mx(

@@ -26,7 +26,6 @@ TILES_PER_HALF = HALF // JT
 ROW0, ROW1 = 96, 112
 TAB_AT, WER_AT, WEI_AT, WR_AT, TAB2_AT = 0, J, J + R, J + 2 * R, J + 3 * R
 ODD_WIDTH, EVEN_WIDTH = TAB2_AT, TAB2_AT + J
-QUANT_LAG = 2
 AHEAD = 2
 
 
@@ -55,8 +54,8 @@ def tile_list_ckg_bias_kernel(
 
         nc.vector.memset(tab_s[0:ROW0, :], 0)
         nc.vector.memset(tab2_s[:], 0)
-        nc.gpsimd.memset(odd[:], 0)
-        nc.gpsimd.memset(even[:], 0)
+        nc.vector.memset(odd[:], 0)
+        nc.vector.memset(even[:], 0)
 
         nc.sync.dma_start(idx[:], offs)
         nc.sync.dma_start(out=tab_s[ROW0:, :], in_=tab_scales.rearrange("a q t -> (a q) t").bitcast(I32))
@@ -109,8 +108,8 @@ def tile_list_ckg_bias_kernel(
 
         got_w = raw.tile([P, J], U32, name="got_w", tag="then_got_w", align_bytes=64)
         got2_w = []
-        parted = keep.tile([P, 2, 2, 2 * HALF], U8, name="parted", align_bytes=64)
-        we = keep.tile([P, 2, 2, R], I32, name="we", align_bytes=64)
+        parted = raw.tile([P, 2, 2, 2 * HALF], U8, name="parted", tag="then_n_codes", align_bytes=64)
+        we = raw.tile([P, 2, 2, R], I32, name="we", tag="then_codes", align_bytes=64)
         wr = keep.tile([P, 2, R // 2], I32, name="wr", align_bytes=64)
 
         def entity_words(half):
@@ -181,27 +180,30 @@ def tile_list_ckg_bias_kernel(
                 accs.append(acc)
             return accs
 
-        def products(ent, accs):
+        def products(ent, accs, real_first):
             arr, ari = (acc[:].rearrange("p t j -> p j t") for acc in accs)
             with_re = work.tile([P, 2, JT, PACK], F32, name="with_re", tag="with_re")
             with_im = work.tile([P, 2, JT, PACK], F32, name="with_im", tag="with_im")
-            nc.vector.tensor_tensor(
-                out=with_re[:], in0=ent[:], in1=arr.unsqueeze(1).to_broadcast([P, 2, JT, PACK]), op=MULT
-            )
+            if real_first:
+                nc.vector.tensor_tensor(out=with_re[:, 0, :, :], in0=ent[:, 0, :, :], in1=arr, op=MULT)
+            else:
+                nc.vector.tensor_tensor(
+                    out=with_re[:], in0=ent[:], in1=arr.unsqueeze(1).to_broadcast([P, 2, JT, PACK]), op=MULT
+                )
             nc.vector.scalar_tensor_tensor(
                 out=with_im[:, 0, :, :], in0=ent[:, 1, :, :], scalar=-1.0, in1=ari, op0=MULT, op1=MULT
             )
+            if real_first:
+                nc.vector.tensor_tensor(out=with_re[:, 1, :, :], in0=ent[:, 1, :, :], in1=arr, op=MULT)
             nc.vector.tensor_tensor(out=with_im[:, 1, :, :], in0=ent[:, 0, :, :], in1=ari, op=MULT)
             return with_re, with_im
 
-        def complex_sum(adder, prods):
-            h = work.tile([P, 2 * JT * PACK], BF16, name="h", tag="h", align_bytes=64, bufs=4)
-            flat = [prod[:].rearrange("p m j t -> p (m j t)") for prod in prods]
-            adder.tensor_tensor(out=h[:], in0=flat[0], in1=flat[1], op=ADD)
-            return h
+        def complex_sum(adder, prods, h, slot, parts=slice(0, 2)):
+            flat = [prod[:, parts, :, :].rearrange("p m j t -> p m (j t)") for prod in prods]
+            adder.tensor_tensor(out=h[:, parts, slot, :], in0=flat[0], in1=flat[1], op=ADD)
 
-        n_codes = keep.tile([P, 2, N], U32, name="n_codes", align_bytes=64)
-        n_scales = keep.tile([P, 2, N], U8, name="n_scales", align_bytes=64)
+        def h_tile(count, tag):
+            return raw.tile([P, 2, count, JT * PACK], BF16, name="h", tag=tag, align_bytes=64)
 
         n_bf = keep.tile([P, 2, 2, P, PACK], BF16, name="n_bf", align_bytes=64)
 
@@ -209,51 +211,66 @@ def tile_list_ckg_bias_kernel(
             for part in range(2):
                 nc.scalar.copy(out=n_bf[:, part, :, :, :], in_=n_raw[:, part, :, :].rearrange("p t (m h) -> p h m t", h=2))
 
-        def quantise_candidates():
-            nc.vector.quantize_mx(
-                out=n_codes[:].rearrange("p m n -> p (m n)").bitcast(FP8X4),
-                scales=n_scales[:].rearrange("p m n -> p (m n)"),
-                in_=n_bf[:].rearrange("p a h m t -> p (a h m t)"),
-            )
+        def quantise(name, values, tag):
+            width = values.shape[1] // PACK
+            codes = raw.tile([P, width], U32, name=name + "_codes", tag=tag, align_bytes=64)
+            scales = keep.tile([P, width], U8, name=name + "_scales", align_bytes=64)
+            nc.vector.quantize_mx(out=codes[:].bitcast(FP8X4), scales=scales[:], in_=values)
+            return codes, scales
 
-        def scores(i, h):
-            codes = work.tile([P, 2 * JT], U32, name="codes", tag="codes", align_bytes=64)
-            scales = work.tile([P, 2 * JT], U8, name="scales", tag="scales", align_bytes=64)
-            nc.vector.quantize_mx(out=codes[:].bitcast(FP8X4), scales=scales[:], in_=h[:])
-            acc = psum.tile([P, 2, JT], F32, name="acc_y", tag="acc_y", bufs=2)
-            y = work.tile([P, 2, JT], F32, name="y", tag="y")
+        out_rows = out.rearrange("(p h) j -> p h j", h=2)
+
+        def scores(first, h, tag, share=False):
+            width = h.shape[2] * JT
+            codes, scales = quantise("h%d" % first, h[:].rearrange("p m i c -> p (m i c)"), tag)
+            y = keep.tile([P, 2, width], F32, name="y%d" % first)
             for nh in range(2):
+                acc = psum.tile([P, width], F32, name="acc_y", tag="acc_y", bufs=2)
                 for part in range(2):
+                    n_cols = slice(part * N + nh * P, part * N + (nh + 1) * P)
+                    h_cols = slice(part * width, (part + 1) * width)
                     nc.tensor.matmul_mx(
-                        out=acc[:, nh, :],
-                        lhsT=n_codes[:, part, nh * P : (nh + 1) * P].bitcast(FP8X4),
-                        lhsT_scale=n_scales[:, part, nh * P : (nh + 1) * P],
-                        rhs=codes[:, part * JT : (part + 1) * JT].bitcast(FP8X4),
-                        rhs_scale=scales[:, part * JT : (part + 1) * JT],
+                        out=acc[:],
+                        lhsT=n_codes[:, n_cols].bitcast(FP8X4),
+                        lhsT_scale=n_scales[:, n_cols],
+                        rhs=codes[:, h_cols].bitcast(FP8X4),
+                        rhs_scale=scales[:, h_cols],
                         start=(part == 0),
                         stop=(part == 1),
                     )
-            for nh in range(2):
-                nc.scalar.activation(out=y[:, nh, :], in_=acc[:, nh, :], func=IDENTITY, bias=bias[:, nh : nh + 1])
-            nc.sync.dma_start(out=out.rearrange("(p h) j -> p h j", h=2)[:, :, i * JT : (i + 1) * JT], in_=y[:])
+                if share and nh == 1:
+                    nc.vector.tensor_scalar_add(out=y[:, nh, :], in0=acc[:], scalar1=bias[:, nh : nh + 1])
+                else:
+                    nc.scalar.activation(out=y[:, nh, :], in_=acc[:], func=IDENTITY, bias=bias[:, nh : nh + 1])
+            nc.sync.dma_start(out=out_rows[:, :, first * JT : first * JT + width], in_=y[:])
 
         ents = [entity(i) for i in range(AHEAD)]
         rels = [relation(0)]
-        hs = []
         last = TILES - 1
+        h_a, h_b = h_tile(4, "h_a"), h_tile(1, "h_b")
         for i in range(TILES):
             if i < last:
                 rels.append(relation(i + 1))
-            prods = products(ents[i], rels[i])
-            if i < last:
-                hs.append(complex_sum(nc.gpsimd, prods))
+            prods = products(ents[i], rels[i], i == 0)
             if i + AHEAD < TILES:
                 ents.append(entity(i + AHEAD))
-            if i == QUANT_LAG - 1:
+            if i == 1:
                 round_candidates()
-            if i == QUANT_LAG:
-                quantise_candidates()
-            if i >= QUANT_LAG:
-                scores(i - QUANT_LAG, hs[i - QUANT_LAG])
-        scores(last - 1, hs[last - 1])
-        scores(last, complex_sum(nc.vector, prods))
+            if i == 5:
+                n_codes, n_scales = quantise("n", n_bf[:].rearrange("p a h m t -> p (a h m t)"), "then_n_codes")
+                scores(0, h_a, "then_codes")
+                h_c = h_tile(2, "h_a")
+            if i == 0:
+                complex_sum(nc.gpsimd, prods, h_a, i, slice(0, 1))
+                complex_sum(nc.gpsimd, prods, h_a, i, slice(1, 2))
+            elif i < 4:
+                complex_sum(nc.gpsimd, prods, h_a, i)
+            elif i == 4:
+                complex_sum(nc.gpsimd, prods, h_b, 0)
+            elif i < last:
+                complex_sum(nc.gpsimd, prods, h_c, i - 5)
+        scores(4, h_b, "codes_b")
+        scores(5, h_c, "codes_c")
+        h_d = h_tile(1, "h_d")
+        complex_sum(nc.vector, prods, h_d, 0)
+        scores(last, h_d, "codes_d", share=True)

@@ -54,8 +54,8 @@ def tile_list_ckg_bias_kernel(
 
         nc.vector.memset(tab_s[0:ROW0, :], 0)
         nc.vector.memset(tab2_s[:], 0)
-        nc.vector.memset(odd[:], 0)
-        nc.vector.memset(even[:], 0)
+        nc.gpsimd.memset(odd[:], 0)
+        nc.gpsimd.memset(even[:], 0)
 
         nc.sync.dma_start(idx[:], offs)
         nc.sync.dma_start(out=tab_s[ROW0:, :], in_=tab_scales.rearrange("a q t -> (a q) t").bitcast(I32))
@@ -108,8 +108,8 @@ def tile_list_ckg_bias_kernel(
 
         got_w = raw.tile([P, J], U32, name="got_w", tag="then_got_w", align_bytes=64)
         got2_w = []
-        parted = raw.tile([P, 2, 2, 2 * HALF], U8, name="parted", tag="then_n_codes", align_bytes=64)
-        we = raw.tile([P, 2, 2, R], I32, name="we", tag="then_codes", align_bytes=64)
+        parted = keep.tile([P, 2, 2, 2 * HALF], U8, name="parted", align_bytes=64)
+        we = keep.tile([P, 2, 2, R], I32, name="we", align_bytes=64)
         wr = keep.tile([P, 2, R // 2], I32, name="wr", align_bytes=64)
 
         def entity_words(half):
@@ -202,75 +202,77 @@ def tile_list_ckg_bias_kernel(
             flat = [prod[:, parts, :, :].rearrange("p m j t -> p m (j t)") for prod in prods]
             adder.tensor_tensor(out=h[:, parts, slot, :], in0=flat[0], in1=flat[1], op=ADD)
 
-        def h_tile(count, tag):
-            return raw.tile([P, 2, count, JT * PACK], BF16, name="h", tag=tag, align_bytes=64)
+        def h_view(values):
+            return values.rearrange("p (m i c) -> p m i c", m=2, c=JT * PACK)
 
-        n_bf = keep.tile([P, 2, 2, P, PACK], BF16, name="n_bf", align_bytes=64)
-
-        def round_candidates():
-            for part in range(2):
-                nc.scalar.copy(out=n_bf[:, part, :, :, :], in_=n_raw[:, part, :, :].rearrange("p t (m h) -> p h m t", h=2))
-
-        def quantise(name, values, tag):
+        def quantise(name, values):
             width = values.shape[1] // PACK
-            codes = raw.tile([P, width], U32, name=name + "_codes", tag=tag, align_bytes=64)
+            codes = keep.tile([P, width], U32, name=name + "_codes", align_bytes=64)
             scales = keep.tile([P, width], U8, name=name + "_scales", align_bytes=64)
             nc.vector.quantize_mx(out=codes[:].bitcast(FP8X4), scales=scales[:], in_=values)
-            return codes, scales
+            return codes[:], scales[:]
 
         out_rows = out.rearrange("(p h) j -> p h j", h=2)
 
-        def scores(first, h, tag, share=False):
-            width = h.shape[2] * JT
-            codes, scales = quantise("h%d" % first, h[:].rearrange("p m i c -> p (m i c)"), tag)
+        def scores(first, n_mx, h_mx):
+            width = h_mx[0].shape[1] // 2
             y = keep.tile([P, 2, width], F32, name="y%d" % first)
             for nh in range(2):
-                acc = psum.tile([P, width], F32, name="acc_y", tag="acc_y", bufs=2)
+                tag, bufs = {6: ("acc_e", 2), 7: ("acc_r", 4)}.get(first, ("acc_y", 2))
+                acc = psum.tile([P, width], F32, name="acc_y", tag=tag, bufs=bufs)
                 for part in range(2):
                     n_cols = slice(part * N + nh * P, part * N + (nh + 1) * P)
                     h_cols = slice(part * width, (part + 1) * width)
                     nc.tensor.matmul_mx(
                         out=acc[:],
-                        lhsT=n_codes[:, n_cols].bitcast(FP8X4),
-                        lhsT_scale=n_scales[:, n_cols],
-                        rhs=codes[:, h_cols].bitcast(FP8X4),
-                        rhs_scale=scales[:, h_cols],
+                        lhsT=n_mx[0][:, n_cols].bitcast(FP8X4),
+                        lhsT_scale=n_mx[1][:, n_cols],
+                        rhs=h_mx[0][:, h_cols].bitcast(FP8X4),
+                        rhs_scale=h_mx[1][:, h_cols],
                         start=(part == 0),
                         stop=(part == 1),
                     )
-                if share and nh == 1:
+                if first == TILES - 1 and nh == 1:
                     nc.vector.tensor_scalar_add(out=y[:, nh, :], in0=acc[:], scalar1=bias[:, nh : nh + 1])
                 else:
                     nc.scalar.activation(out=y[:, nh, :], in_=acc[:], func=IDENTITY, bias=bias[:, nh : nh + 1])
             nc.sync.dma_start(out=out_rows[:, :, first * JT : first * JT + width], in_=y[:])
 
+        tile_width = 2 * JT * PACK
+        n_width = 2 * N * PACK
+        n_flat = keep.tile([P, n_width], BF16, name="n_flat", align_bytes=64)
+        n_values = n_flat[:].rearrange("p (a h m t) -> p a h m t", a=2, h=2, t=PACK)
+        h_values = {0: keep.tile([P, 2 * tile_width], BF16, name="h0", align_bytes=64)[:]}
+        for first in range(2, TILES):
+            h_values[first] = keep.tile([P, tile_width], BF16, name="h%d" % first, align_bytes=64)[:]
+
         ents = [entity(i) for i in range(AHEAD)]
         rels = [relation(0)]
         last = TILES - 1
-        h_a, h_b = h_tile(4, "h_a"), h_tile(1, "h_b")
         for i in range(TILES):
             if i < last:
                 rels.append(relation(i + 1))
             prods = products(ents[i], rels[i], i == 0)
+            if i == 0:
+                complex_sum(nc.gpsimd, prods, h_view(h_values[0]), 0, slice(0, 1))
+                complex_sum(nc.gpsimd, prods, h_view(h_values[0]), 0, slice(1, 2))
+            elif i == 1:
+                complex_sum(nc.gpsimd, prods, h_view(h_values[0]), 1)
+            elif i < last:
+                complex_sum(nc.gpsimd, prods, h_view(h_values[i]), 0)
             if i + AHEAD < TILES:
                 ents.append(entity(i + AHEAD))
             if i == 1:
-                round_candidates()
-            if i == 5:
-                n_codes, n_scales = quantise("n", n_bf[:].rearrange("p a h m t -> p (a h m t)"), "then_n_codes")
-                scores(0, h_a, "then_codes")
-                h_c = h_tile(2, "h_a")
-            if i == 0:
-                complex_sum(nc.gpsimd, prods, h_a, i, slice(0, 1))
-                complex_sum(nc.gpsimd, prods, h_a, i, slice(1, 2))
-            elif i < 4:
-                complex_sum(nc.gpsimd, prods, h_a, i)
-            elif i == 4:
-                complex_sum(nc.gpsimd, prods, h_b, 0)
-            elif i < last:
-                complex_sum(nc.gpsimd, prods, h_c, i - 5)
-        scores(4, h_b, "codes_b")
-        scores(5, h_c, "codes_c")
-        h_d = h_tile(1, "h_d")
-        complex_sum(nc.vector, prods, h_d, 0)
-        scores(last, h_d, "codes_d", share=True)
+                for part in range(2):
+                    nc.scalar.copy(
+                        out=n_values[:, part, :, :, :], in_=n_raw[:, part, :, :].rearrange("p t (m h) -> p h m t", h=2)
+                    )
+            if i == 2:
+                n_mx = quantise("n", n_flat[:])
+            if i == 3:
+                scores(0, n_mx, quantise("h0", h_values[0]))
+            if i > 3:
+                scores(i - 2, n_mx, quantise("h%d" % (i - 2), h_values[i - 2]))
+        scores(last - 1, n_mx, quantise("h6", h_values[last - 1]))
+        complex_sum(nc.vector, prods, h_view(h_values[last]), 0)
+        scores(last, n_mx, quantise("h7", h_values[last]))

@@ -24,9 +24,8 @@ TILES = J // JT
 HALF = J // 2
 TILES_PER_HALF = HALF // JT
 ROW0, ROW1 = 96, 112
-TAB_AT, WER_AT, WEI_AT, WR_AT, TAB2_AT = 0, J, J + R, J + 2 * R, J + 3 * R
-ODD_WIDTH, EVEN_WIDTH = TAB2_AT, TAB2_AT + J
-AHEAD = 2
+AHEAD = 3
+PLANE = J + 2 * R
 
 
 def tile_list_ckg_bias_kernel(
@@ -37,173 +36,176 @@ def tile_list_ckg_bias_kernel(
     with ExitStack() as ctx:
         keep = ctx.enter_context(tc.tile_pool(name="keep", bufs=1))
         raw = ctx.enter_context(tc.tile_pool(name="raw", bufs=1))
-        work = ctx.enter_context(tc.tile_pool(name="work", bufs=3))
+        work = ctx.enter_context(tc.tile_pool(name="work", bufs=4))
         psum = ctx.enter_context(tc.psum_pool(name="psum", bufs=2))
 
         idx = keep.tile([P, J // 16], U16, name="idx")
         idx2 = keep.tile([P, J // 16], U16, name="idx2")
-        tab_s = keep.tile([P, T // 4], I32, name="tab_s", align_bytes=64)
-        tab2_s = keep.tile([P, T // 4], I32, name="tab2_s", align_bytes=64)
-        tab_w = raw.tile([P, T], I32, name="tab_w", tag="then_candidates", align_bytes=64)
-        w_s_raw = keep.tile([P, 3, R // 4], I32, name="w_s_raw", align_bytes=64)
-        staged = keep.tile([P, EVEN_WIDTH // 4], I32, name="staged", align_bytes=64)
-        even = keep.tile([P, EVEN_WIDTH // 4], I32, name="even", align_bytes=64)
-        odd = keep.tile([P, ODD_WIDTH // 4], I32, name="odd", align_bytes=64)
+        tab_s = raw.tile([P, T // 4], I32, name="tab_s", tag="then_staged_e", align_bytes=64)
+        tab2_s = raw.tile([P, T // 4], I32, name="tab2_s", tag="then_staged_r", align_bytes=64)
+        tab2_w = keep.tile([P, T], I32, name="tab2_w", align_bytes=64)
+        wr_raw = keep.tile([P, 2, R // 2], I32, name="wr_raw", align_bytes=64)
+        wr_s_raw = raw.tile([P, 2, R // 4], I32, name="wr_s_raw", tag="then_tab", align_bytes=64)
+        we_s_raw = raw.tile([P, 2, R // 4], I32, name="we_s_raw", tag="then_wei", align_bytes=64)
+        plane_r = keep.tile([P, PLANE // 4], I32, name="plane_r", align_bytes=64)
+        plane_e = keep.tile([P, 2, PLANE // 4], I32, name="plane_e", align_bytes=64)
         bias_raw = keep.tile([P, 2], F32, name="bias_raw")
         bias = keep.tile([P, 2], F32, name="bias")
 
+        nc.vector.memset(tab2_s[0:ROW1, :], 0)
         nc.vector.memset(tab_s[0:ROW0, :], 0)
-        nc.vector.memset(tab2_s[:], 0)
-        nc.gpsimd.memset(odd[:], 0)
-        nc.gpsimd.memset(even[:], 0)
+        nc.gpsimd.memset(wr_s_raw[ROW0:ROW1, :, :], 0)
+        nc.gpsimd.memset(plane_r[:], 0)
 
+        nc.sync.dma_start(idx2[:], offs2)
+        nc.sync.dma_start(out=tab2_s[ROW1:, :], in_=tab2_scales[0].bitcast(I32))
         nc.sync.dma_start(idx[:], offs)
         nc.sync.dma_start(out=tab_s[ROW0:, :], in_=tab_scales.rearrange("a q t -> (a q) t").bitcast(I32))
-        nc.sync.dma_start(idx2[:], offs2)
-        nc.scalar.dma_start(out=w_s_raw[ROW0:, 0, :], in_=wer_scales.rearrange("a q r -> (a q) r").bitcast(I32))
-        nc.scalar.dma_start(out=w_s_raw[ROW0:, 1, :], in_=wei_scales.rearrange("a q r -> (a q) r").bitcast(I32))
-        nc.scalar.dma_start(out=w_s_raw[ROW0:ROW1, 2, :], in_=wrr_scales[0].bitcast(I32))
-        nc.scalar.dma_start(out=w_s_raw[ROW1:, 2, :], in_=wri_scales[0].bitcast(I32))
-        tab_rows = tab_words[0].rearrange("p t i -> p (t i)").bitcast(I32)
-        nc.sync.dma_start(out=tab_w[:, : T // 2], in_=tab_rows[:, : T // 2])
-        nc.sync.dma_start(out=tab2_s[ROW0:ROW1, :], in_=tab2_scales[0].bitcast(I32))
-        nc.sync.dma_start(out=tab_w[:, T // 2 :], in_=tab_rows[:, T // 2 :])
+        for part, scales in enumerate((wrr_scales, wri_scales)):
+            nc.scalar.dma_start(out=wr_s_raw[ROW1:, part, :], in_=scales[0].bitcast(I32))
+        nc.sync.dma_start(out=tab2_w[:], in_=tab2_words[0].rearrange("p t i -> p (t i)").bitcast(I32))
+        for part, words in enumerate((wrr_words, wri_words)):
+            nc.sync.dma_start(out=wr_raw[:, part, :], in_=words[0].bitcast(I32))
+        we_raw = []
+
+        def load_entity_weight(words, tag):
+            w_raw = raw.tile([P, 2, R], I32, name="we_raw", tag=tag, align_bytes=64)
+            nc.sync.dma_start(out=w_raw[:], in_=words.rearrange("a p r i -> p a (r i)").bitcast(I32))
+            we_raw.append(w_raw)
+
+        load_entity_weight(wer_words, "wer")
+        for part, scales in enumerate((wer_scales, wei_scales)):
+            nc.gpsimd.dma_start(out=we_s_raw[ROW0:, part, :], in_=scales.rearrange("a q r -> (a q) r").bitcast(I32))
         nc.gpsimd.dma_start(out=bias_raw[:], in_=b.rearrange("(p h) -> p h", h=2))
+        nc.gpsimd.memset(plane_e[:], 0)
         nc.scalar.activation(out=bias[:], in_=bias_raw[:], func=IDENTITY)
 
-        got_s = raw.tile([P, J], U8, name="got_s", tag="then_we", align_bytes=64)
+        def stage_scales(name, table_s, offsets, w_s_raws):
+            got = raw.tile([P, J], U8, name="got_" + name, tag="then_got2_w", align_bytes=64)
+            nc.vector.tensor_copy(got[:], table_s[:].bitcast(U8).indirect(offsets[:]))
+            staged = raw.tile([P, PLANE // 4], I32, name="staged_" + name, tag="then_staged_" + name, align_bytes=64)
+            nc.vector.tensor_copy(out=staged[ROW0:, 0 : J // 4], in_=got[ROW0:, :].bitcast(I32))
+            at = J // 4
+            for w_s_raw in w_s_raws:
+                width = w_s_raw.shape[1] * R // 4
+                nc.vector.tensor_copy(
+                    out=staged[ROW0:, at : at + width].rearrange("p (m t g w) -> p m t g w", t=PACK, g=16, w=2),
+                    in_=w_s_raw[ROW0:, :, :].rearrange("p m (g t w) -> p m t g w", t=PACK, w=2),
+                )
+                at = at + width
+            return staged
+
+        staged_r = stage_scales("r", tab2_s, idx2, [wr_s_raw])
+        for r in range(4):
+            nc.sync.dma_start(out=plane_r[r:P:32, :], in_=staged_r[ROW1 + r : P : 4, :])
+        tab_w = raw.tile([P, T], I32, name="tab_w", tag="then_tab", align_bytes=64)
+        nc.sync.dma_start(out=tab_w[:], in_=tab_words[0].rearrange("p t i -> p (t i)").bitcast(I32))
+        staged_e = stage_scales("e", tab_s, idx, [we_s_raw])
+        load_entity_weight(wei_words, "then_wei")
+        for a in range(2):
+            for r in range(4):
+                first = ROW0 + 16 * a
+                nc.sync.dma_start(out=plane_e[r:P:32, a, :], in_=staged_e[first + r : first + 16 : 4, :])
+
         halves = [
             (slice(half * HALF, (half + 1) * HALF), slice(half * HALF // 16, (half + 1) * HALF // 16))
             for half in range(2)
         ]
-        for cols, entries in halves:
-            nc.vector.tensor_copy(got_s[:, cols], tab_s[:].bitcast(U8).indirect(idx[:, entries]))
-        nc.vector.tensor_copy(
-            out=staged[ROW0:, WER_AT // 4 : TAB2_AT // 4].rearrange("p (m t g w) -> p m t g w", m=3, t=PACK, w=2),
-            in_=w_s_raw[ROW0:, :, :].rearrange("p m (g t w) -> p m t g w", t=PACK, w=2),
-        )
-        nc.vector.tensor_copy(out=staged[ROW0:, TAB_AT // 4 : WER_AT // 4], in_=got_s[ROW0:, :].bitcast(I32))
-        for r in range(4):
-            nc.sync.dma_start(out=odd[r:P:32, :], in_=staged[ROW1 + r : P : 4, 0 : ODD_WIDTH // 4])
-        w_raw = raw.tile([P, 5, R], I32, name="w_raw", tag="then_we", align_bytes=64)
-        we_raw = w_raw[:, 0:4, :].rearrange("p (m a) r -> p m a r", a=2)
-        wr_raw = w_raw[:, 4, :].rearrange("p (m w) -> p m w", m=2)
-        for part, words in enumerate((wer_words, wei_words)):
-            nc.sync.dma_start(out=we_raw[:, part, :, :], in_=words.rearrange("a p r i -> p a (r i)").bitcast(I32))
-        for part, words in enumerate((wrr_words, wri_words)):
-            nc.sync.dma_start(out=wr_raw[:, part, :], in_=words[0].bitcast(I32))
-        got2_s = []
-        for (cols, entries), tag in zip(halves, ("then_got_w", "then_tab2")):
-            got = raw.tile([P, HALF], U8, name="got2_s", tag=tag, align_bytes=64)
-            nc.vector.tensor_copy(got[:], tab2_s[:].bitcast(U8).indirect(idx2[:, entries]))
-            got2_s.append(got)
-        for half, got in enumerate(got2_s):
-            at = (TAB2_AT + half * HALF) // 4
-            nc.vector.tensor_copy(out=staged[ROW0:, at : at + HALF // 4], in_=got[ROW0:, :].bitcast(I32))
-        for r in range(4):
-            nc.sync.dma_start(out=even[r:P:32, :], in_=staged[ROW0 + r : ROW1 : 4, :])
-        planes = (even[:].bitcast(U8), odd[:].bitcast(U8))
-        tab2_w = raw.tile([P, T], I32, name="tab2_w", tag="then_tab2", align_bytes=64)
-        nc.sync.dma_start(out=tab2_w[:], in_=tab2_words[0].rearrange("p t i -> p (t i)").bitcast(I32))
-
-        got_w = raw.tile([P, J], U32, name="got_w", tag="then_got_w", align_bytes=64)
-        got2_w = []
-        parted = keep.tile([P, 2, 2, 2 * HALF], U8, name="parted", align_bytes=64)
-        we = keep.tile([P, 2, 2, R], I32, name="we", align_bytes=64)
         wr = keep.tile([P, 2, R // 2], I32, name="wr", align_bytes=64)
+        nc.vector.tensor_copy(
+            out=wr[:].rearrange("p m (t g w) -> p m t g w", t=PACK, w=4),
+            in_=wr_raw[:].rearrange("p m (g t w) -> p m t g w", t=PACK, w=4),
+        )
+        got2_w = []
+        for (cols, entries), tag in zip(halves, ("then_got2_w", "then_staged_r")):
+            got = raw.tile([P, HALF], U32, name="got2_w", tag=tag, align_bytes=64)
+            nc.vector.tensor_copy(got[:], tab2_w[:].bitcast(U32).indirect(idx2[:, entries]))
+            got2_w.append(got)
 
-        def entity_words(half):
-            cols, entries = halves[half]
+        scales_r = plane_r[:].bitcast(U8)
+
+        def relation(i):
+            half, at = divmod(i * JT, HALF)
+            rel = work.tile([P, 3, JT, PACK], F32, name="rel", tag="rel", bufs=AHEAD)
+            for part in range(2):
+                acc = psum.tile([P, PACK, JT], F32, name="acc_r", tag="acc_r", bufs=2)
+                w_at = J + part * R
+                for t in range(PACK):
+                    nc.tensor.matmul_mx(
+                        out=acc[:, t, :],
+                        lhsT=wr[:, part, t * P // 2 : (t + 1) * P // 2].bitcast(FP4X4),
+                        lhsT_scale=scales_r[:, w_at + t * P : w_at + (t + 1) * P],
+                        rhs=got2_w[half][:, at : at + JT].bitcast(FP8X4),
+                        rhs_scale=scales_r[:, i * JT : (i + 1) * JT],
+                        start=True,
+                        stop=True,
+                    )
+                nc.scalar.copy(out=rel[:, 1 + part, :, :], in_=acc[:].rearrange("p t j -> p j t"))
+            return rel
+
+        def negate(rel):
+            nc.scalar.mul(out=rel[:, 0, :, :], in_=rel[:, 2, :, :], mul=-1.0)
+
+        rels = [relation(i) for i in range(AHEAD)]
+        for rel in rels[:2]:
+            negate(rel)
+
+        we = keep.tile([P, 2, 2, R], I32, name="we", align_bytes=64)
+
+        def order_weights(part):
+            nc.vector.tensor_copy(
+                out=we[:, part, :, :].rearrange("p a (t g q) -> p a t g q", t=PACK, q=8),
+                in_=we_raw[part][:].rearrange("p a (g t q) -> p a t g q", t=PACK, q=8),
+            )
+
+        order_weights(0)
+        got_w = keep.tile([P, J], U32, name="got_w", align_bytes=64)
+        parted = keep.tile([P, 2, 2, 2 * HALF], U8, name="parted", align_bytes=64)
+        for half, (cols, entries) in enumerate(halves):
             nc.vector.tensor_copy(got_w[:, cols], tab_w[:].bitcast(U32).indirect(idx[:, entries]))
             nc.vector.tensor_copy(
                 out=parted[:, half, :, :].bitcast(U16),
                 in_=got_w[:, cols].bitcast(U16).rearrange("p (j d) -> p d j", d=2),
             )
-
-        def relation_words(half):
-            got = keep.tile([P, HALF], U32, name="got2_w%d" % half, align_bytes=64)
-            nc.vector.tensor_copy(got[:], tab2_w[:].bitcast(U32).indirect(idx2[:, halves[half][1]]))
-            got2_w.append(got)
-
-        entity_words(0)
-        for part in range(2):
-            nc.vector.tensor_copy(
-                out=we[:, part, :, :].rearrange("p a (t g q) -> p a t g q", t=PACK, q=8),
-                in_=we_raw[:, part, :, :].rearrange("p a (g t q) -> p a t g q", t=PACK, q=8),
-            )
-        nc.vector.tensor_copy(
-            out=wr[:].rearrange("p m (t g w) -> p m t g w", t=PACK, w=4),
-            in_=wr_raw.rearrange("p m (g t w) -> p m t g w", t=PACK, w=4),
-        )
-        entity_words(1)
-        n_raw = raw.tile([P, 2, PACK, N], F32, name="n_raw", tag="then_candidates", align_bytes=64)
+            if half == 0:
+                order_weights(1)
+        n_raw = raw.tile([P, 2, PACK, N], F32, name="n_raw", tag="then_tab", align_bytes=64)
         for part, mat in enumerate((nr, ni)):
             for t in range(PACK):
                 nc.sync.dma_start(out=n_raw[:, part, t, :], in_=mat.rearrange("(g t q) n -> t g q n", t=PACK, q=8)[t])
-        relation_words(0)
-        relation_words(1)
 
-        def entity(i):
+        def entity(i, part):
             half, at = divmod(i * JT, HALF)
-            ent = work.tile([P, 2, JT, PACK], F32, name="ent", tag="ent", bufs=AHEAD)
-            for part, w_at in enumerate((WER_AT, WEI_AT)):
-                acc = psum.tile([P, PACK, JT], F32, name="acc_e", tag="acc_e", bufs=2)
-                for t in range(PACK):
-                    for a in range(2):
-                        nc.tensor.matmul_mx(
-                            out=acc[:, t, :],
-                            lhsT=we[:, part, a, t * P : (t + 1) * P].bitcast(FP8X4),
-                            lhsT_scale=planes[a][:, w_at + t * P : w_at + (t + 1) * P],
-                            rhs=parted[:, half, a, 2 * at : 2 * (at + JT)].bitcast(FP4X4),
-                            rhs_scale=planes[a][:, TAB_AT + i * JT : TAB_AT + (i + 1) * JT],
-                            start=(a == 0),
-                            stop=(a == 1),
-                        )
-                nc.scalar.copy(out=ent[:, part, :, :], in_=acc[:].rearrange("p t j -> p j t"))
-            return ent
-
-        def relation(i):
-            half, at = divmod(i * JT, HALF)
-            accs = []
-            for part in range(2):
-                acc = psum.tile([P, PACK, JT], F32, name="acc_r", tag="acc_r", bufs=4)
-                for t in range(PACK):
+            acc = psum.tile([P, PACK, JT], F32, name="acc_e", tag="acc_e", bufs=4)
+            w_at = J + part * R
+            for t in range(PACK):
+                for a in range(2):
+                    scales_e = plane_e[:, a, :].bitcast(U8)
                     nc.tensor.matmul_mx(
                         out=acc[:, t, :],
-                        lhsT=wr[:, part, t * P // 2 : (t + 1) * P // 2].bitcast(FP4X4),
-                        lhsT_scale=planes[part][:, WR_AT + t * P : WR_AT + (t + 1) * P],
-                        rhs=got2_w[half][:, at : at + JT].bitcast(FP8X4),
-                        rhs_scale=planes[0][:, TAB2_AT + i * JT : TAB2_AT + (i + 1) * JT],
-                        start=True,
-                        stop=True,
+                        lhsT=we[:, part, a, t * P : (t + 1) * P].bitcast(FP8X4),
+                        lhsT_scale=scales_e[:, w_at + t * P : w_at + (t + 1) * P],
+                        rhs=parted[:, half, a, 2 * at : 2 * (at + JT)].bitcast(FP4X4),
+                        rhs_scale=scales_e[:, i * JT : (i + 1) * JT],
+                        start=(a == 0),
+                        stop=(a == 1),
                     )
-                accs.append(acc)
-            return accs
+            return acc[:].rearrange("p t j -> p j t")
 
-        def products(ent, accs, real_first):
-            arr, ari = (acc[:].rearrange("p t j -> p j t") for acc in accs)
-            with_re = work.tile([P, 2, JT, PACK], F32, name="with_re", tag="with_re")
-            with_im = work.tile([P, 2, JT, PACK], F32, name="with_im", tag="with_im")
-            if real_first:
-                nc.vector.tensor_tensor(out=with_re[:, 0, :, :], in0=ent[:, 0, :, :], in1=arr, op=MULT)
-            else:
-                nc.vector.tensor_tensor(
-                    out=with_re[:], in0=ent[:], in1=arr.unsqueeze(1).to_broadcast([P, 2, JT, PACK]), op=MULT
-                )
-            nc.vector.scalar_tensor_tensor(
-                out=with_im[:, 0, :, :], in0=ent[:, 1, :, :], scalar=-1.0, in1=ari, op0=MULT, op1=MULT
+        def product(prod, rel, acc, part, terms=slice(0, 2)):
+            count = terms.stop - terms.start
+            at = 1 - part + terms.start
+            nc.vector.tensor_tensor(
+                out=prod[:, terms, :, :],
+                in0=rel[:, at : at + count, :, :],
+                in1=acc.unsqueeze(1).to_broadcast([P, count, JT, PACK]),
+                op=MULT,
             )
-            if real_first:
-                nc.vector.tensor_tensor(out=with_re[:, 1, :, :], in0=ent[:, 1, :, :], in1=arr, op=MULT)
-            nc.vector.tensor_tensor(out=with_im[:, 1, :, :], in0=ent[:, 0, :, :], in1=ari, op=MULT)
-            return with_re, with_im
 
         def complex_sum(adder, prods, h, slot, parts=slice(0, 2)):
             flat = [prod[:, parts, :, :].rearrange("p m j t -> p m (j t)") for prod in prods]
-            adder.tensor_tensor(out=h[:, parts, slot, :], in0=flat[0], in1=flat[1], op=ADD)
-
-        def h_view(values):
-            return values.rearrange("p (m i c) -> p m i c", m=2, c=JT * PACK)
+            h_view = h.rearrange("p (m i c) -> p m i c", m=2, c=JT * PACK)
+            adder.tensor_tensor(out=h_view[:, parts, slot, :], in0=flat[0], in1=flat[1], op=ADD)
 
         def quantise(name, values):
             width = values.shape[1] // PACK
@@ -218,8 +220,8 @@ def tile_list_ckg_bias_kernel(
             width = h_mx[0].shape[1] // 2
             y = keep.tile([P, 2, width], F32, name="y%d" % first)
             for nh in range(2):
-                tag, bufs = {6: ("acc_e", 2), 7: ("acc_r", 4)}.get(first, ("acc_y", 2))
-                acc = psum.tile([P, width], F32, name="acc_y", tag=tag, bufs=bufs)
+                tag = "acc_r" if first == TILES - 1 else "acc_y"
+                acc = psum.tile([P, width], F32, name="acc_y", tag=tag, bufs=2)
                 for part in range(2):
                     n_cols = slice(part * N + nh * P, part * N + (nh + 1) * P)
                     h_cols = slice(part * width, (part + 1) * width)
@@ -239,40 +241,51 @@ def tile_list_ckg_bias_kernel(
             nc.sync.dma_start(out=out_rows[:, :, first * JT : first * JT + width], in_=y[:])
 
         tile_width = 2 * JT * PACK
-        n_width = 2 * N * PACK
-        n_flat = keep.tile([P, n_width], BF16, name="n_flat", align_bytes=64)
+        n_flat = keep.tile([P, 2 * N * PACK], BF16, name="n_flat", align_bytes=64)
         n_values = n_flat[:].rearrange("p (a h m t) -> p a h m t", a=2, h=2, t=PACK)
-        h_values = {0: keep.tile([P, 2 * tile_width], BF16, name="h0", align_bytes=64)[:]}
-        for first in range(2, TILES):
+        last = TILES - 1
+        h_values = {}
+        for first in range(0, last - 1, 2):
+            h_values[first] = keep.tile([P, 2 * tile_width], BF16, name="h%d" % first, align_bytes=64)[:]
+        for first in (last - 1, last):
             h_values[first] = keep.tile([P, tile_width], BF16, name="h%d" % first, align_bytes=64)[:]
 
-        ents = [entity(i) for i in range(AHEAD)]
-        rels = [relation(0)]
-        last = TILES - 1
+        real, imag = slice(0, 1), slice(1, 2)
+        all_prods = []
         for i in range(TILES):
-            if i < last:
-                rels.append(relation(i + 1))
-            prods = products(ents[i], rels[i], i == 0)
+            with_re = work.tile([P, 2, JT, PACK], F32, name="with_re", tag="with_re")
+            with_im = work.tile([P, 2, JT, PACK], F32, name="with_im", tag="with_im")
+            prods = (with_re, with_im)
+            all_prods.append(prods)
+            product(with_re, rels[i], entity(i, 0), 0)
             if i == 0:
-                complex_sum(nc.gpsimd, prods, h_view(h_values[0]), 0, slice(0, 1))
-                complex_sum(nc.gpsimd, prods, h_view(h_values[0]), 0, slice(1, 2))
-            elif i == 1:
-                complex_sum(nc.gpsimd, prods, h_view(h_values[0]), 1)
-            elif i < last:
-                complex_sum(nc.gpsimd, prods, h_view(h_values[i]), 0)
+                aei = entity(i, 1)
+                for terms in (real, imag):
+                    product(with_im, rels[i], aei, 1, terms)
+                    complex_sum(nc.gpsimd, prods, h_values[0], 0, terms)
+            else:
+                product(with_im, rels[i], entity(i, 1), 1)
+            if 0 < i < last - 1:
+                complex_sum(nc.gpsimd, prods, h_values[i - i % 2], i % 2)
+            if i == last - 1:
+                complex_sum(nc.gpsimd, prods, h_values[i], 0, real)
+            if i + 2 < TILES:
+                negate(rels[i + 2])
             if i + AHEAD < TILES:
-                ents.append(entity(i + AHEAD))
+                rels.append(relation(i + AHEAD))
             if i == 1:
                 for part in range(2):
                     nc.scalar.copy(
                         out=n_values[:, part, :, :, :], in_=n_raw[:, part, :, :].rearrange("p t (m h) -> p h m t", h=2)
                     )
-            if i == 2:
-                n_mx = quantise("n", n_flat[:])
             if i == 3:
+                n_mx = quantise("n", n_flat[:])
+            if i == 4:
                 scores(0, n_mx, quantise("h0", h_values[0]))
-            if i > 3:
-                scores(i - 2, n_mx, quantise("h%d" % (i - 2), h_values[i - 2]))
+            if i == 5:
+                scores(2, n_mx, quantise("h2", h_values[2]))
+        scores(4, n_mx, quantise("h4", h_values[4]))
+        complex_sum(nc.vector, all_prods[last - 1], h_values[last - 1], 0, imag)
+        complex_sum(nc.vector, all_prods[last], h_values[last], 0)
         scores(last - 1, n_mx, quantise("h6", h_values[last - 1]))
-        complex_sum(nc.vector, prods, h_view(h_values[last]), 0)
         scores(last, n_mx, quantise("h7", h_values[last]))

@@ -1,6 +1,7 @@
 from contextlib import ExitStack
 
 import concourse.mybir as mybir
+from concourse.masks import make_identity
 
 K, L, R, N, T, J = 1024, 512, 512, 256, 4096, 1024
 FLOPS = 2 * J * (2 * K * R + 2 * L * R + 2 * R * N)
@@ -25,6 +26,7 @@ HALF = J // 2
 TILES_PER_HALF = HALF // JT
 ROW0, ROW1 = 96, 112
 AHEAD = 3
+TURNED = (6, 7)
 PLANE = J + 2 * R
 
 
@@ -54,8 +56,12 @@ def tile_list_ckg_bias_kernel(
 
         nc.vector.memset(tab2_s[0:ROW1, :], 0)
         nc.vector.memset(tab_s[0:ROW0, :], 0)
-        nc.gpsimd.memset(wr_s_raw[ROW0:ROW1, :, :], 0)
-        nc.gpsimd.memset(plane_r[:], 0)
+        nc.vector.memset(wr_s_raw[ROW0:ROW1, :, :], 0)
+        nc.vector.memset(plane_r[:], 0)
+        nc.gpsimd.dma_start(out=bias_raw[:], in_=b.rearrange("(p h) -> p h", h=2))
+        nc.gpsimd.memset(plane_e[:], 0)
+        identity = keep.tile([P, P], F32, name="identity")
+        make_identity(nc, identity[:])
 
         nc.sync.dma_start(idx2[:], offs2)
         nc.sync.dma_start(out=tab2_s[ROW1:, :], in_=tab2_scales[0].bitcast(I32))
@@ -66,6 +72,8 @@ def tile_list_ckg_bias_kernel(
         nc.sync.dma_start(out=tab2_w[:], in_=tab2_words[0].rearrange("p t i -> p (t i)").bitcast(I32))
         for part, words in enumerate((wrr_words, wri_words)):
             nc.sync.dma_start(out=wr_raw[:, part, :], in_=words[0].bitcast(I32))
+        for part, scales in enumerate((wer_scales, wei_scales)):
+            nc.sync.dma_start(out=we_s_raw[ROW0:, part, :], in_=scales.rearrange("a q r -> (a q) r").bitcast(I32))
         we_raw = []
 
         def load_entity_weight(words, tag):
@@ -74,10 +82,6 @@ def tile_list_ckg_bias_kernel(
             we_raw.append(w_raw)
 
         load_entity_weight(wer_words, "wer")
-        for part, scales in enumerate((wer_scales, wei_scales)):
-            nc.gpsimd.dma_start(out=we_s_raw[ROW0:, part, :], in_=scales.rearrange("a q r -> (a q) r").bitcast(I32))
-        nc.gpsimd.dma_start(out=bias_raw[:], in_=b.rearrange("(p h) -> p h", h=2))
-        nc.gpsimd.memset(plane_e[:], 0)
         nc.scalar.activation(out=bias[:], in_=bias_raw[:], func=IDENTITY)
 
         def stage_scales(name, table_s, offsets, w_s_raws):
@@ -105,7 +109,8 @@ def tile_list_ckg_bias_kernel(
         for a in range(2):
             for r in range(4):
                 first = ROW0 + 16 * a
-                nc.sync.dma_start(out=plane_e[r:P:32, a, :], in_=staged_e[first + r : first + 16 : 4, :])
+                queue = nc.gpsimd if 4 * a + r >= 6 else nc.sync
+                queue.dma_start(out=plane_e[r:P:32, a, :], in_=staged_e[first + r : first + 16 : 4, :])
 
         halves = [
             (slice(half * HALF, (half + 1) * HALF), slice(half * HALF // 16, (half + 1) * HALF // 16))
@@ -124,47 +129,70 @@ def tile_list_ckg_bias_kernel(
 
         scales_r = plane_r[:].bitcast(U8)
 
+        def lanes_last(acc, i):
+            if i in TURNED:
+                return acc[:]
+            return acc[:].rearrange("p (t j) -> p j t", t=PACK)
+
+        def like_sums(values, i):
+            if i in TURNED:
+                return values
+            return values.rearrange("p m (j t) -> p m j t", t=PACK)
+
         def relation(i):
             half, at = divmod(i * JT, HALF)
-            rel = work.tile([P, 3, JT, PACK], F32, name="rel", tag="rel", bufs=AHEAD)
+            rel = work.tile([P, 3, R], F32, name="rel", tag="rel", bufs=AHEAD)
+            picked = got2_w[half][:, at : at + JT].bitcast(FP8X4)
+            picked_scale = scales_r[:, i * JT : (i + 1) * JT]
             for part in range(2):
-                acc = psum.tile([P, PACK, JT], F32, name="acc_r", tag="acc_r", bufs=2)
+                acc = psum.tile([P, R], F32, name="acc_r", tag="acc_r", bufs=2)
                 w_at = J + part * R
-                for t in range(PACK):
+                if i in TURNED:
                     nc.tensor.matmul_mx(
-                        out=acc[:, t, :],
-                        lhsT=wr[:, part, t * P // 2 : (t + 1) * P // 2].bitcast(FP4X4),
-                        lhsT_scale=scales_r[:, w_at + t * P : w_at + (t + 1) * P],
-                        rhs=got2_w[half][:, at : at + JT].bitcast(FP8X4),
-                        rhs_scale=scales_r[:, i * JT : (i + 1) * JT],
+                        out=acc[:],
+                        lhsT=picked,
+                        lhsT_scale=picked_scale,
+                        rhs=wr[:, part, :].bitcast(FP4X4),
+                        rhs_scale=scales_r[:, w_at : w_at + R],
                         start=True,
                         stop=True,
                     )
-                nc.scalar.copy(out=rel[:, 1 + part, :, :], in_=acc[:].rearrange("p t j -> p j t"))
+                else:
+                    for t in range(PACK):
+                        nc.tensor.matmul_mx(
+                            out=acc[:, t * JT : (t + 1) * JT],
+                            lhsT=wr[:, part, t * P // 2 : (t + 1) * P // 2].bitcast(FP4X4),
+                            lhsT_scale=scales_r[:, w_at + t * P : w_at + (t + 1) * P],
+                            rhs=picked,
+                            rhs_scale=picked_scale,
+                            start=True,
+                            stop=True,
+                        )
+                nc.scalar.copy(out=like_sums(rel[:], i)[:, 1 + part], in_=lanes_last(acc, i))
             return rel
 
         def negate(rel):
-            nc.scalar.mul(out=rel[:, 0, :, :], in_=rel[:, 2, :, :], mul=-1.0)
+            nc.scalar.mul(out=rel[:, 0, :], in_=rel[:, 2, :], mul=-1.0)
 
         rels = [relation(i) for i in range(AHEAD)]
         for rel in rels[:2]:
             negate(rel)
 
-        we = keep.tile([P, 2, 2, R], I32, name="we", align_bytes=64)
+        we = [keep.tile([P, 2, R], I32, name="we%d" % part, align_bytes=64) for part in range(2)]
 
         def order_weights(part):
             nc.vector.tensor_copy(
-                out=we[:, part, :, :].rearrange("p a (t g q) -> p a t g q", t=PACK, q=8),
+                out=we[part][:].rearrange("p a (t g q) -> p a t g q", t=PACK, q=8),
                 in_=we_raw[part][:].rearrange("p a (g t q) -> p a t g q", t=PACK, q=8),
             )
 
         order_weights(0)
         got_w = keep.tile([P, J], U32, name="got_w", align_bytes=64)
-        parted = keep.tile([P, 2, 2, 2 * HALF], U8, name="parted", align_bytes=64)
+        parted = [keep.tile([P, 2, 2 * HALF], U8, name="parted%d" % half, align_bytes=64) for half in range(2)]
         for half, (cols, entries) in enumerate(halves):
             nc.vector.tensor_copy(got_w[:, cols], tab_w[:].bitcast(U32).indirect(idx[:, entries]))
             nc.vector.tensor_copy(
-                out=parted[:, half, :, :].bitcast(U16),
+                out=parted[half][:].bitcast(U16),
                 in_=got_w[:, cols].bitcast(U16).rearrange("p (j d) -> p d j", d=2),
             )
             if half == 0:
@@ -176,36 +204,64 @@ def tile_list_ckg_bias_kernel(
 
         def entity(i, part):
             half, at = divmod(i * JT, HALF)
-            acc = psum.tile([P, PACK, JT], F32, name="acc_e", tag="acc_e", bufs=4)
+            acc = psum.tile([P, R], F32, name="acc_e", tag="acc_e", bufs=4)
             w_at = J + part * R
-            for t in range(PACK):
+            picked = [parted[half][:, a, 2 * at : 2 * (at + JT)].bitcast(FP4X4) for a in range(2)]
+            scales_e = [plane_e[:, a, :].bitcast(U8) for a in range(2)]
+            if i in TURNED:
                 for a in range(2):
-                    scales_e = plane_e[:, a, :].bitcast(U8)
                     nc.tensor.matmul_mx(
-                        out=acc[:, t, :],
-                        lhsT=we[:, part, a, t * P : (t + 1) * P].bitcast(FP8X4),
-                        lhsT_scale=scales_e[:, w_at + t * P : w_at + (t + 1) * P],
-                        rhs=parted[:, half, a, 2 * at : 2 * (at + JT)].bitcast(FP4X4),
-                        rhs_scale=scales_e[:, i * JT : (i + 1) * JT],
+                        out=acc[:],
+                        lhsT=picked[a],
+                        lhsT_scale=scales_e[a][:, i * JT : (i + 1) * JT],
+                        rhs=we[part][:, a, :].bitcast(FP8X4),
+                        rhs_scale=scales_e[a][:, w_at : w_at + R],
                         start=(a == 0),
                         stop=(a == 1),
                     )
-            return acc[:].rearrange("p t j -> p j t")
+            else:
+                for t in range(PACK):
+                    for a in range(2):
+                        nc.tensor.matmul_mx(
+                            out=acc[:, t * JT : (t + 1) * JT],
+                            lhsT=we[part][:, a, t * P : (t + 1) * P].bitcast(FP8X4),
+                            lhsT_scale=scales_e[a][:, w_at + t * P : w_at + (t + 1) * P],
+                            rhs=picked[a],
+                            rhs_scale=scales_e[a][:, i * JT : (i + 1) * JT],
+                            start=(a == 0),
+                            stop=(a == 1),
+                        )
+            return lanes_last(acc, i)
 
-        def product(prod, rel, acc, part, terms=slice(0, 2)):
+        def product(i, prod, rel, acc, part, terms=slice(0, 2)):
             count = terms.stop - terms.start
             at = 1 - part + terms.start
             nc.vector.tensor_tensor(
-                out=prod[:, terms, :, :],
-                in0=rel[:, at : at + count, :, :],
-                in1=acc.unsqueeze(1).to_broadcast([P, count, JT, PACK]),
+                out=like_sums(prod[:], i)[:, terms],
+                in0=like_sums(rel[:], i)[:, at : at + count],
+                in1=acc.unsqueeze(1).to_broadcast([P, count] + list(acc.shape[1:])),
                 op=MULT,
             )
 
         def complex_sum(adder, prods, h, slot, parts=slice(0, 2)):
-            flat = [prod[:, parts, :, :].rearrange("p m j t -> p m (j t)") for prod in prods]
             h_view = h.rearrange("p (m i c) -> p m i c", m=2, c=JT * PACK)
-            adder.tensor_tensor(out=h_view[:, parts, slot, :], in0=flat[0], in1=flat[1], op=ADD)
+            adder.tensor_tensor(out=h_view[:, parts, slot, :], in0=prods[0][:, parts, :], in1=prods[1][:, parts, :], op=ADD)
+
+        def turned_sum(prods, h, part):
+            acc = psum.tile([P, PACK, JT], F32, name="acc_h", tag="acc_r", bufs=2)
+            for term, prod in enumerate(prods):
+                for t in range(PACK):
+                    nc.tensor.matmul(
+                        out=acc[:, t, :],
+                        lhsT=prod[:, part, t * P : (t + 1) * P],
+                        rhs=identity[:],
+                        is_transpose=True,
+                        start=(term == 0 and t == 0),
+                        stop=(term == 1 and t == PACK - 1),
+                    )
+            nc.scalar.copy(
+                out=h.rearrange("p (m j t) -> p m j t", m=2, t=PACK)[:, part], in_=acc[:].rearrange("p t j -> p j t")
+            )
 
         def quantise(name, values):
             width = values.shape[1] // PACK
@@ -220,8 +276,8 @@ def tile_list_ckg_bias_kernel(
             width = h_mx[0].shape[1] // 2
             y = keep.tile([P, 2, width], F32, name="y%d" % first)
             for nh in range(2):
-                tag = "acc_r" if first == TILES - 1 else "acc_y"
-                acc = psum.tile([P, width], F32, name="acc_y", tag=tag, bufs=2)
+                tag, bufs = ("acc_e", 4) if first == TILES - 1 else ("acc_y", 2)
+                acc = psum.tile([P, width], F32, name="acc_y", tag=tag, bufs=bufs)
                 for part in range(2):
                     n_cols = slice(part * N + nh * P, part * N + (nh + 1) * P)
                     h_cols = slice(part * width, (part + 1) * width)
@@ -251,24 +307,24 @@ def tile_list_ckg_bias_kernel(
             h_values[first] = keep.tile([P, tile_width], BF16, name="h%d" % first, align_bytes=64)[:]
 
         real, imag = slice(0, 1), slice(1, 2)
-        all_prods = []
         for i in range(TILES):
-            with_re = work.tile([P, 2, JT, PACK], F32, name="with_re", tag="with_re")
-            with_im = work.tile([P, 2, JT, PACK], F32, name="with_im", tag="with_im")
+            with_re = work.tile([P, 2, R], F32, name="with_re", tag="with_re")
+            with_im = work.tile([P, 2, R], F32, name="with_im", tag="with_im")
             prods = (with_re, with_im)
-            all_prods.append(prods)
-            product(with_re, rels[i], entity(i, 0), 0)
-            if i == 0:
-                aei = entity(i, 1)
+            product(i, with_re, rels[i], entity(i, 0), 0)
+            aei = entity(i, 1)
+            if i in (0, last):
                 for terms in (real, imag):
-                    product(with_im, rels[i], aei, 1, terms)
-                    complex_sum(nc.gpsimd, prods, h_values[0], 0, terms)
+                    product(i, with_im, rels[i], aei, 1, terms)
+                    if i == 0:
+                        complex_sum(nc.gpsimd, prods, h_values[0], 0, terms)
             else:
-                product(with_im, rels[i], entity(i, 1), 1)
-            if 0 < i < last - 1:
+                product(i, with_im, rels[i], aei, 1)
+            if i in TURNED:
+                for part in range(2):
+                    turned_sum(prods, h_values[i], part)
+            elif i > 0:
                 complex_sum(nc.gpsimd, prods, h_values[i - i % 2], i % 2)
-            if i == last - 1:
-                complex_sum(nc.gpsimd, prods, h_values[i], 0, real)
             if i + 2 < TILES:
                 negate(rels[i + 2])
             if i + AHEAD < TILES:
@@ -284,8 +340,5 @@ def tile_list_ckg_bias_kernel(
                 scores(0, n_mx, quantise("h0", h_values[0]))
             if i == 5:
                 scores(2, n_mx, quantise("h2", h_values[2]))
-        scores(4, n_mx, quantise("h4", h_values[4]))
-        complex_sum(nc.vector, all_prods[last - 1], h_values[last - 1], 0, imag)
-        complex_sum(nc.vector, all_prods[last], h_values[last], 0)
-        scores(last - 1, n_mx, quantise("h6", h_values[last - 1]))
-        scores(last, n_mx, quantise("h7", h_values[last]))
+        for first in (4, last - 1, last):
+            scores(first, n_mx, quantise("h%d" % first, h_values[first]))

@@ -26,7 +26,7 @@ HALF = J // 2
 TILES_PER_HALF = HALF // JT
 ROW0, ROW1 = 96, 112
 AHEAD = 3
-TURNED = (6, 7)
+TURNED = (7,)
 PLANE = J + 2 * R
 
 
@@ -58,10 +58,12 @@ def tile_list_ckg_bias_kernel(
         nc.vector.memset(tab_s[0:ROW0, :], 0)
         nc.vector.memset(wr_s_raw[ROW0:ROW1, :, :], 0)
         nc.vector.memset(plane_r[:], 0)
-        nc.gpsimd.dma_start(out=bias_raw[:], in_=b.rearrange("(p h) -> p h", h=2))
         nc.gpsimd.memset(plane_e[:], 0)
         identity = keep.tile([P, P], F32, name="identity")
         make_identity(nc, identity[:])
+        for part, scales in enumerate((wer_scales, wei_scales)):
+            nc.gpsimd.dma_start(out=we_s_raw[ROW0:, part, :], in_=scales.rearrange("a q r -> (a q) r").bitcast(I32))
+        nc.gpsimd.dma_start(out=bias_raw[:], in_=b.rearrange("(p h) -> p h", h=2))
 
         nc.sync.dma_start(idx2[:], offs2)
         nc.sync.dma_start(out=tab2_s[ROW1:, :], in_=tab2_scales[0].bitcast(I32))
@@ -72,8 +74,6 @@ def tile_list_ckg_bias_kernel(
         nc.sync.dma_start(out=tab2_w[:], in_=tab2_words[0].rearrange("p t i -> p (t i)").bitcast(I32))
         for part, words in enumerate((wrr_words, wri_words)):
             nc.sync.dma_start(out=wr_raw[:, part, :], in_=words[0].bitcast(I32))
-        for part, scales in enumerate((wer_scales, wei_scales)):
-            nc.sync.dma_start(out=we_s_raw[ROW0:, part, :], in_=scales.rearrange("a q r -> (a q) r").bitcast(I32))
         we_raw = []
 
         def load_entity_weight(words, tag):
@@ -109,8 +109,7 @@ def tile_list_ckg_bias_kernel(
         for a in range(2):
             for r in range(4):
                 first = ROW0 + 16 * a
-                queue = nc.gpsimd if 4 * a + r >= 6 else nc.sync
-                queue.dma_start(out=plane_e[r:P:32, a, :], in_=staged_e[first + r : first + 16 : 4, :])
+                nc.sync.dma_start(out=plane_e[r:P:32, a, :], in_=staged_e[first + r : first + 16 : 4, :])
 
         halves = [
             (slice(half * HALF, (half + 1) * HALF), slice(half * HALF // 16, (half + 1) * HALF // 16))
@@ -204,7 +203,7 @@ def tile_list_ckg_bias_kernel(
 
         def entity(i, part):
             half, at = divmod(i * JT, HALF)
-            acc = psum.tile([P, R], F32, name="acc_e", tag="acc_e", bufs=4)
+            acc = psum.tile([P, R], F32, name="acc_e", tag="acc_e", bufs=3)
             w_at = J + part * R
             picked = [parted[half][:, a, 2 * at : 2 * (at + JT)].bitcast(FP4X4) for a in range(2)]
             scales_e = [plane_e[:, a, :].bitcast(U8) for a in range(2)]
@@ -272,21 +271,29 @@ def tile_list_ckg_bias_kernel(
 
         out_rows = out.rearrange("(p h) j -> p h j", h=2)
 
+        def quantise_h(first):
+            values = h_values[first]
+            width = values.shape[1] // 2
+            if first == TILES - 1:
+                return [quantise("h%d_%d" % (first, part), values[:, part * width : (part + 1) * width]) for part in range(2)]
+            codes, scales = quantise("h%d" % first, values)
+            words = width // PACK
+            return [(codes[:, part * words : (part + 1) * words], scales[:, part * words : (part + 1) * words]) for part in range(2)]
+
         def scores(first, n_mx, h_mx):
-            width = h_mx[0].shape[1] // 2
+            width = h_mx[0][0].shape[1]
             y = keep.tile([P, 2, width], F32, name="y%d" % first)
             for nh in range(2):
-                tag, bufs = ("acc_e", 4) if first == TILES - 1 else ("acc_y", 2)
+                tag, bufs = ("acc_e", 3) if first == TILES - 1 else ("acc_y", 3)
                 acc = psum.tile([P, width], F32, name="acc_y", tag=tag, bufs=bufs)
                 for part in range(2):
                     n_cols = slice(part * N + nh * P, part * N + (nh + 1) * P)
-                    h_cols = slice(part * width, (part + 1) * width)
                     nc.tensor.matmul_mx(
                         out=acc[:],
                         lhsT=n_mx[0][:, n_cols].bitcast(FP8X4),
                         lhsT_scale=n_mx[1][:, n_cols],
-                        rhs=h_mx[0][:, h_cols].bitcast(FP8X4),
-                        rhs_scale=h_mx[1][:, h_cols],
+                        rhs=h_mx[part][0].bitcast(FP8X4),
+                        rhs_scale=h_mx[part][1],
                         start=(part == 0),
                         stop=(part == 1),
                     )
@@ -294,7 +301,12 @@ def tile_list_ckg_bias_kernel(
                     nc.vector.tensor_scalar_add(out=y[:, nh, :], in0=acc[:], scalar1=bias[:, nh : nh + 1])
                 else:
                     nc.scalar.activation(out=y[:, nh, :], in_=acc[:], func=IDENTITY, bias=bias[:, nh : nh + 1])
-            nc.sync.dma_start(out=out_rows[:, :, first * JT : first * JT + width], in_=y[:])
+            cols = slice(first * JT, first * JT + width)
+            if first == TILES - 1:
+                for nh, queue in enumerate((nc.scalar, nc.sync)):
+                    queue.dma_start(out=out_rows[:, nh, cols], in_=y[:, nh, :])
+            else:
+                nc.sync.dma_start(out=out_rows[:, :, cols], in_=y[:])
 
         tile_width = 2 * JT * PACK
         n_flat = keep.tile([P, 2 * N * PACK], BF16, name="n_flat", align_bytes=64)
@@ -311,20 +323,21 @@ def tile_list_ckg_bias_kernel(
             with_re = work.tile([P, 2, R], F32, name="with_re", tag="with_re")
             with_im = work.tile([P, 2, R], F32, name="with_im", tag="with_im")
             prods = (with_re, with_im)
-            product(i, with_re, rels[i], entity(i, 0), 0)
-            aei = entity(i, 1)
-            if i in (0, last):
+            aer, aei = entity(i, 0), entity(i, 1)
+            if i == 0:
                 for terms in (real, imag):
+                    product(i, with_re, rels[i], aer, 0, terms)
                     product(i, with_im, rels[i], aei, 1, terms)
-                    if i == 0:
-                        complex_sum(nc.gpsimd, prods, h_values[0], 0, terms)
+                    complex_sum(nc.gpsimd, prods, h_values[0], 0, terms)
             else:
-                product(i, with_im, rels[i], aei, 1)
+                product(i, with_re, rels[i], aer, 0)
+                for terms in (real, imag) if i == last else (slice(0, 2),):
+                    product(i, with_im, rels[i], aei, 1, terms)
             if i in TURNED:
                 for part in range(2):
                     turned_sum(prods, h_values[i], part)
             elif i > 0:
-                complex_sum(nc.gpsimd, prods, h_values[i - i % 2], i % 2)
+                complex_sum(nc.gpsimd, prods, h_values[i - i % 2], i % 2 if i < last - 1 else 0)
             if i + 2 < TILES:
                 negate(rels[i + 2])
             if i + AHEAD < TILES:
@@ -337,8 +350,8 @@ def tile_list_ckg_bias_kernel(
             if i == 3:
                 n_mx = quantise("n", n_flat[:])
             if i == 4:
-                scores(0, n_mx, quantise("h0", h_values[0]))
-            if i == 5:
-                scores(2, n_mx, quantise("h2", h_values[2]))
+                scores(0, n_mx, quantise_h(0))
+            if i == 6:
+                scores(2, n_mx, quantise_h(2))
         for first in (4, last - 1, last):
-            scores(first, n_mx, quantise("h%d" % first, h_values[first]))
+            scores(first, n_mx, quantise_h(first))

@@ -25,8 +25,8 @@ TILES = J // JT
 HALF = J // 2
 TILES_PER_HALF = HALF // JT
 ROW0, ROW1 = 96, 112
-AHEAD = 3
-TURNED = (7,)
+AHEAD = 5
+TURNED = (3, 7)
 PLANE = J + 2 * R
 
 
@@ -46,7 +46,7 @@ def tile_list_ckg_bias_kernel(
         tab_s = raw.tile([P, T // 4], I32, name="tab_s", tag="then_staged_e", align_bytes=64)
         tab2_s = raw.tile([P, T // 4], I32, name="tab2_s", tag="then_staged_r", align_bytes=64)
         tab2_w = keep.tile([P, T], I32, name="tab2_w", align_bytes=64)
-        wr_raw = keep.tile([P, 2, R // 2], I32, name="wr_raw", align_bytes=64)
+        wr_raw = raw.tile([P, 2, R // 2], I32, name="wr_raw", tag="then_second", align_bytes=64)
         wr_s_raw = raw.tile([P, 2, R // 4], I32, name="wr_s_raw", tag="then_tab", align_bytes=64)
         we_s_raw = raw.tile([P, 2, R // 4], I32, name="we_s_raw", tag="then_wei", align_bytes=64)
         plane_r = keep.tile([P, PLANE // 4], I32, name="plane_r", align_bytes=64)
@@ -84,12 +84,18 @@ def tile_list_ckg_bias_kernel(
         load_entity_weight(wer_words, "wer")
         nc.scalar.activation(out=bias[:], in_=bias_raw[:], func=IDENTITY)
 
-        def stage_scales(name, table_s, offsets, w_s_raws):
-            got = raw.tile([P, J], U8, name="got_" + name, tag="then_got2_w", align_bytes=64)
-            nc.vector.tensor_copy(got[:], table_s[:].bitcast(U8).indirect(offsets[:]))
+        def gather_scales(table_s, offsets, tag):
+            got = raw.tile([P, 16 * offsets.shape[1]], U8, name="got_s", tag=tag, align_bytes=64)
+            nc.vector.tensor_copy(got[:], table_s[:].bitcast(U8).indirect(offsets))
+            return got
+
+        def stage_scales(name, gots, w_s_raws):
             staged = raw.tile([P, PLANE // 4], I32, name="staged_" + name, tag="then_staged_" + name, align_bytes=64)
-            nc.vector.tensor_copy(out=staged[ROW0:, 0 : J // 4], in_=got[ROW0:, :].bitcast(I32))
-            at = J // 4
+            at = 0
+            for got in gots:
+                width = got.shape[1] // 4
+                nc.vector.tensor_copy(out=staged[ROW0:, at : at + width], in_=got[ROW0:, :].bitcast(I32))
+                at = at + width
             for w_s_raw in w_s_raws:
                 width = w_s_raw.shape[1] * R // 4
                 nc.vector.tensor_copy(
@@ -99,32 +105,37 @@ def tile_list_ckg_bias_kernel(
                 at = at + width
             return staged
 
-        staged_r = stage_scales("r", tab2_s, idx2, [wr_s_raw])
+        staged_r = stage_scales("r", [gather_scales(tab2_s, idx2[:], "then_first")], [wr_s_raw])
         for r in range(4):
             nc.sync.dma_start(out=plane_r[r:P:32, :], in_=staged_r[ROW1 + r : P : 4, :])
         tab_w = raw.tile([P, T], I32, name="tab_w", tag="then_tab", align_bytes=64)
         nc.sync.dma_start(out=tab_w[:], in_=tab_words[0].rearrange("p t i -> p (t i)").bitcast(I32))
-        staged_e = stage_scales("e", tab_s, idx, [we_s_raw])
-        load_entity_weight(wei_words, "then_wei")
-        for a in range(2):
-            for r in range(4):
-                first = ROW0 + 16 * a
-                nc.sync.dma_start(out=plane_e[r:P:32, a, :], in_=staged_e[first + r : first + 16 : 4, :])
-
         halves = [
             (slice(half * HALF, (half + 1) * HALF), slice(half * HALF // 16, (half + 1) * HALF // 16))
             for half in range(2)
         ]
+        got_s = [gather_scales(tab_s, idx[:, halves[0][1]], "then_first")]
+        got2_w = []
+
+        def gather_relation_words(half, tag):
+            got = raw.tile([P, HALF], U32, name="got2_w", tag=tag, align_bytes=64)
+            nc.vector.tensor_copy(got[:], tab2_w[:].bitcast(U32).indirect(idx2[:, halves[half][1]]))
+            got2_w.append(got)
+
+        gather_relation_words(0, "got2_first")
         wr = keep.tile([P, 2, R // 2], I32, name="wr", align_bytes=64)
         nc.vector.tensor_copy(
             out=wr[:].rearrange("p m (t g w) -> p m t g w", t=PACK, w=4),
             in_=wr_raw[:].rearrange("p m (g t w) -> p m t g w", t=PACK, w=4),
         )
-        got2_w = []
-        for (cols, entries), tag in zip(halves, ("then_got2_w", "then_staged_r")):
-            got = raw.tile([P, HALF], U32, name="got2_w", tag=tag, align_bytes=64)
-            nc.vector.tensor_copy(got[:], tab2_w[:].bitcast(U32).indirect(idx2[:, entries]))
-            got2_w.append(got)
+        got_s.append(gather_scales(tab_s, idx[:, halves[1][1]], "then_second"))
+        staged_e = stage_scales("e", got_s, [we_s_raw])
+        for a in range(2):
+            for r in range(4):
+                first = ROW0 + 16 * a
+                nc.sync.dma_start(out=plane_e[r:P:32, a, :], in_=staged_e[first + r : first + 16 : 4, :])
+        load_entity_weight(wei_words, "then_wei")
+        gather_relation_words(1, "then_second")
 
         scales_r = plane_r[:].bitcast(U8)
 
@@ -144,7 +155,7 @@ def tile_list_ckg_bias_kernel(
             picked = got2_w[half][:, at : at + JT].bitcast(FP8X4)
             picked_scale = scales_r[:, i * JT : (i + 1) * JT]
             for part in range(2):
-                acc = psum.tile([P, R], F32, name="acc_r", tag="acc_r", bufs=2)
+                acc = psum.tile([P, R], F32, name="acc_r", tag="acc_r", bufs=3)
                 w_at = J + part * R
                 if i in TURNED:
                     nc.tensor.matmul_mx(
@@ -177,16 +188,17 @@ def tile_list_ckg_bias_kernel(
         for rel in rels[:2]:
             negate(rel)
 
-        we = [keep.tile([P, 2, R], I32, name="we%d" % part, align_bytes=64) for part in range(2)]
+        we = []
 
-        def order_weights(part):
-            nc.vector.tensor_copy(
+        def order_weights(part, engine, tag):
+            we.append(raw.tile([P, 2, R], I32, name="we", tag=tag, align_bytes=64))
+            engine.tensor_copy(
                 out=we[part][:].rearrange("p a (t g q) -> p a t g q", t=PACK, q=8),
                 in_=we_raw[part][:].rearrange("p a (g t q) -> p a t g q", t=PACK, q=8),
             )
 
-        order_weights(0)
-        got_w = keep.tile([P, J], U32, name="got_w", align_bytes=64)
+        order_weights(0, nc.vector, "we0")
+        got_w = raw.tile([P, J], U32, name="got_w", tag="then_we1", align_bytes=64)
         parted = [keep.tile([P, 2, 2 * HALF], U8, name="parted%d" % half, align_bytes=64) for half in range(2)]
         for half, (cols, entries) in enumerate(halves):
             nc.vector.tensor_copy(got_w[:, cols], tab_w[:].bitcast(U32).indirect(idx[:, entries]))
@@ -194,8 +206,7 @@ def tile_list_ckg_bias_kernel(
                 out=parted[half][:].bitcast(U16),
                 in_=got_w[:, cols].bitcast(U16).rearrange("p (j d) -> p d j", d=2),
             )
-            if half == 0:
-                order_weights(1)
+        order_weights(1, nc.gpsimd, "then_we1")
         n_raw = raw.tile([P, 2, PACK, N], F32, name="n_raw", tag="then_tab", align_bytes=64)
         for part, mat in enumerate((nr, ni)):
             for t in range(PACK):
@@ -246,8 +257,8 @@ def tile_list_ckg_bias_kernel(
             h_view = h.rearrange("p (m i c) -> p m i c", m=2, c=JT * PACK)
             adder.tensor_tensor(out=h_view[:, parts, slot, :], in0=prods[0][:, parts, :], in1=prods[1][:, parts, :], op=ADD)
 
-        def turned_sum(prods, h, part):
-            acc = psum.tile([P, PACK, JT], F32, name="acc_h", tag="acc_r", bufs=2)
+        def turned_sum(prods, h, slot, part):
+            acc = psum.tile([P, PACK, JT], F32, name="acc_h", tag="acc_r", bufs=3)
             for term, prod in enumerate(prods):
                 for t in range(PACK):
                     nc.tensor.matmul(
@@ -259,7 +270,8 @@ def tile_list_ckg_bias_kernel(
                         stop=(term == 1 and t == PACK - 1),
                     )
             nc.scalar.copy(
-                out=h.rearrange("p (m j t) -> p m j t", m=2, t=PACK)[:, part], in_=acc[:].rearrange("p t j -> p j t")
+                out=h.rearrange("p (m i j t) -> p m i j t", m=2, j=JT, t=PACK)[:, part, slot],
+                in_=acc[:].rearrange("p t j -> p j t"),
             )
 
         def quantise(name, values):
@@ -284,7 +296,7 @@ def tile_list_ckg_bias_kernel(
             width = h_mx[0][0].shape[1]
             y = keep.tile([P, 2, width], F32, name="y%d" % first)
             for nh in range(2):
-                tag, bufs = ("acc_e", 3) if first == TILES - 1 else ("acc_y", 3)
+                tag, bufs = ("acc_e", 3) if first == TILES - 1 else ("acc_y", 2)
                 acc = psum.tile([P, width], F32, name="acc_y", tag=tag, bufs=bufs)
                 for part in range(2):
                     n_cols = slice(part * N + nh * P, part * N + (nh + 1) * P)
@@ -319,38 +331,48 @@ def tile_list_ckg_bias_kernel(
             h_values[first] = keep.tile([P, tile_width], BF16, name="h%d" % first, align_bytes=64)[:]
 
         real, imag = slice(0, 1), slice(1, 2)
+        early = []
+        for i in range(2):
+            early.append(work.tile([P, 2, R], F32, name="with_re", tag="with_re"))
+            product(i, early[i], rels[i], entity(i, 0), 0)
         for i in range(TILES):
-            with_re = work.tile([P, 2, R], F32, name="with_re", tag="with_re")
+            with_re = early[i] if i < 2 else work.tile([P, 2, R], F32, name="with_re", tag="with_re")
             with_im = work.tile([P, 2, R], F32, name="with_im", tag="with_im")
             prods = (with_re, with_im)
-            aer, aei = entity(i, 0), entity(i, 1)
+            if i >= 2:
+                aer = entity(i, 0)
+            aei = entity(i, 1)
             if i == 0:
                 for terms in (real, imag):
-                    product(i, with_re, rels[i], aer, 0, terms)
                     product(i, with_im, rels[i], aei, 1, terms)
                     complex_sum(nc.gpsimd, prods, h_values[0], 0, terms)
             else:
-                product(i, with_re, rels[i], aer, 0)
+                if i >= 2:
+                    product(i, with_re, rels[i], aer, 0)
+                if i == 4:
+                    n_mx = quantise("n", n_flat[:])
+                    scores(0, n_mx, quantise_h(0))
                 for terms in (real, imag) if i == last else (slice(0, 2),):
                     product(i, with_im, rels[i], aei, 1, terms)
-            if i in TURNED:
+            if i == last:
                 for part in range(2):
-                    turned_sum(prods, h_values[i], part)
+                    turned_sum(prods, h_values[i], 0, part)
+            elif i in TURNED:
+                held = prods
             elif i > 0:
                 complex_sum(nc.gpsimd, prods, h_values[i - i % 2], i % 2 if i < last - 1 else 0)
             if i + 2 < TILES:
                 negate(rels[i + 2])
             if i + AHEAD < TILES:
                 rels.append(relation(i + AHEAD))
+            if i - 2 in TURNED:
+                for part in range(2):
+                    turned_sum(held, h_values[i - 2 - i % 2], i % 2, part)
             if i == 1:
                 for part in range(2):
                     nc.scalar.copy(
                         out=n_values[:, part, :, :, :], in_=n_raw[:, part, :, :].rearrange("p t (m h) -> p h m t", h=2)
                     )
-            if i == 3:
-                n_mx = quantise("n", n_flat[:])
-            if i == 4:
-                scores(0, n_mx, quantise_h(0))
             if i == 6:
                 scores(2, n_mx, quantise_h(2))
         for first in (4, last - 1, last):

@@ -38,7 +38,8 @@ def tile_list_ckg_bias_kernel(
     with ExitStack() as ctx:
         keep = ctx.enter_context(tc.tile_pool(name="keep", bufs=1))
         raw = ctx.enter_context(tc.tile_pool(name="raw", bufs=1))
-        work = ctx.enter_context(tc.tile_pool(name="work", bufs=4))
+        laid = ctx.enter_context(tc.tile_pool(name="laid", bufs=1))
+        work = ctx.enter_context(tc.tile_pool(name="work", bufs=5))
         psum = ctx.enter_context(tc.psum_pool(name="psum", bufs=2))
 
         idx = keep.tile([P, J // 16], U16, name="idx")
@@ -48,7 +49,7 @@ def tile_list_ckg_bias_kernel(
         tab2_w = keep.tile([P, T], I32, name="tab2_w", align_bytes=64)
         wr_raw = raw.tile([P, 2, R // 2], I32, name="wr_raw", tag="then_second", align_bytes=64)
         wr_s_raw = raw.tile([P, 2, R // 4], I32, name="wr_s_raw", tag="then_tab", align_bytes=64)
-        we_s_raw = raw.tile([P, 2, R // 4], I32, name="we_s_raw", tag="then_wei", align_bytes=64)
+        we_s_raw = laid.tile([P, 2, R // 4], I32, name="we_s_raw", offset=4 * R, align_bytes=64)
         plane_r = keep.tile([P, PLANE // 4], I32, name="plane_r", align_bytes=64)
         plane_e = keep.tile([P, 2, PLANE // 4], I32, name="plane_e", align_bytes=64)
         bias_raw = keep.tile([P, 2], F32, name="bias_raw")
@@ -76,12 +77,11 @@ def tile_list_ckg_bias_kernel(
             nc.sync.dma_start(out=wr_raw[:, part, :], in_=words[0].bitcast(I32))
         we_raw = []
 
-        def load_entity_weight(words, tag):
-            w_raw = raw.tile([P, 2, R], I32, name="we_raw", tag=tag, align_bytes=64)
+        def load_entity_weight(words, w_raw):
             nc.sync.dma_start(out=w_raw[:], in_=words.rearrange("a p r i -> p a (r i)").bitcast(I32))
             we_raw.append(w_raw)
 
-        load_entity_weight(wer_words, "wer")
+        load_entity_weight(wer_words, keep.tile([P, 2, R], I32, name="wer_raw", align_bytes=64))
         nc.scalar.activation(out=bias[:], in_=bias_raw[:], func=IDENTITY)
 
         def gather_scales(table_s, offsets, tag):
@@ -134,7 +134,7 @@ def tile_list_ckg_bias_kernel(
             for r in range(4):
                 first = ROW0 + 16 * a
                 nc.sync.dma_start(out=plane_e[r:P:32, a, :], in_=staged_e[first + r : first + 16 : 4, :])
-        load_entity_weight(wei_words, "then_wei")
+        load_entity_weight(wei_words, laid.tile([P, 2, R], I32, name="wei_raw", offset=4 * R, align_bytes=64))
         gather_relation_words(1, "then_second")
 
         scales_r = plane_r[:].bitcast(U8)
@@ -206,7 +206,7 @@ def tile_list_ckg_bias_kernel(
                 out=parted[half][:].bitcast(U16),
                 in_=got_w[:, cols].bitcast(U16).rearrange("p (j d) -> p d j", d=2),
             )
-        order_weights(1, nc.gpsimd, "then_we1")
+        order_weights(1, nc.vector, "then_we1")
         n_raw = raw.tile([P, 2, PACK, N], F32, name="n_raw", tag="then_tab", align_bytes=64)
         for part, mat in enumerate((nr, ni)):
             for t in range(PACK):
@@ -333,8 +333,16 @@ def tile_list_ckg_bias_kernel(
         real, imag = slice(0, 1), slice(1, 2)
         early = []
         for i in range(2):
-            early.append(work.tile([P, 2, R], F32, name="with_re", tag="with_re"))
-            product(i, early[i], rels[i], entity(i, 0), 0)
+            aer = entity(i, 0)
+            early.append(laid.tile([P, 2, R], F32, name="early%d" % i, offset=8 * R * i, align_bytes=64))
+            if i == 0:
+                aer_out = keep.tile([P, R], F32, name="aer_out")
+                nc.scalar.copy(out=aer_out[:].rearrange("p (j t) -> p j t", t=PACK), in_=aer)
+                nc.gpsimd.tensor_tensor(
+                    out=early[i][:], in0=rels[i][:, 1:3, :], in1=aer_out[:].unsqueeze(1).to_broadcast([P, 2, R]), op=MULT
+                )
+            else:
+                product(i, early[i], rels[i], aer, 0)
         for i in range(TILES):
             with_re = early[i] if i < 2 else work.tile([P, 2, R], F32, name="with_re", tag="with_re")
             with_im = work.tile([P, 2, R], F32, name="with_im", tag="with_im")
@@ -342,24 +350,16 @@ def tile_list_ckg_bias_kernel(
             if i >= 2:
                 aer = entity(i, 0)
             aei = entity(i, 1)
-            if i == 0:
-                for terms in (real, imag):
-                    product(i, with_im, rels[i], aei, 1, terms)
-                    complex_sum(nc.gpsimd, prods, h_values[0], 0, terms)
-            else:
-                if i >= 2:
-                    product(i, with_re, rels[i], aer, 0)
-                if i == 4:
-                    n_mx = quantise("n", n_flat[:])
-                    scores(0, n_mx, quantise_h(0))
-                for terms in (real, imag) if i == last else (slice(0, 2),):
-                    product(i, with_im, rels[i], aei, 1, terms)
+            if i >= 2:
+                product(i, with_re, rels[i], aer, 0)
+            for terms in (real, imag) if i == last else (slice(0, 2),):
+                product(i, with_im, rels[i], aei, 1, terms)
             if i == last:
                 for part in range(2):
                     turned_sum(prods, h_values[i], 0, part)
             elif i in TURNED:
                 held = prods
-            elif i > 0:
+            else:
                 complex_sum(nc.gpsimd, prods, h_values[i - i % 2], i % 2 if i < last - 1 else 0)
             if i + 2 < TILES:
                 negate(rels[i + 2])
@@ -373,6 +373,10 @@ def tile_list_ckg_bias_kernel(
                     nc.scalar.copy(
                         out=n_values[:, part, :, :, :], in_=n_raw[:, part, :, :].rearrange("p t (m h) -> p h m t", h=2)
                     )
+            if i == 4:
+                n_mx = quantise("n", n_flat[:])
+            if i == 5:
+                scores(0, n_mx, quantise_h(0))
             if i == 6:
                 scores(2, n_mx, quantise_h(2))
         for first in (4, last - 1, last):

@@ -48,31 +48,28 @@ def tile_list_ckg_bias_kernel(
         tab2_s = raw.tile([P, T // 4], I32, name="tab2_s", tag="then_staged_r", align_bytes=64)
         tab2_w = keep.tile([P, T], I32, name="tab2_w", align_bytes=64)
         wr_raw = raw.tile([P, 2, R // 2], I32, name="wr_raw", tag="then_second", align_bytes=64)
-        wr_s_raw = raw.tile([P, 2, R // 4], I32, name="wr_s_raw", tag="then_tab", align_bytes=64)
+        wr_s_raw = laid.tile([P, 2, R // 4], I32, name="wr_s_raw", offset=23 * R, align_bytes=64)
         we_s_raw = laid.tile([P, 2, R // 4], I32, name="we_s_raw", offset=4 * R, align_bytes=64)
-        plane_r = keep.tile([P, PLANE // 4], I32, name="plane_r", align_bytes=64)
-        plane_e = keep.tile([P, 2, PLANE // 4], I32, name="plane_e", align_bytes=64)
+        plane_e = laid.tile([P, 2, PLANE // 4], I32, name="plane_e", offset=56 * R, align_bytes=64)
         bias_raw = keep.tile([P, 2], F32, name="bias_raw")
         bias = keep.tile([P, 2], F32, name="bias")
 
         nc.vector.memset(tab2_s[0:ROW1, :], 0)
-        nc.vector.memset(tab_s[0:ROW0, :], 0)
-        nc.vector.memset(wr_s_raw[ROW0:ROW1, :, :], 0)
-        nc.vector.memset(plane_r[:], 0)
-        nc.gpsimd.memset(plane_e[:], 0)
-        identity = keep.tile([P, P], F32, name="identity")
-        make_identity(nc, identity[:])
+        nc.vector.memset(wr_s_raw[0:ROW1, :, :], 0)
+        nc.gpsimd.memset(tab_s[0:ROW0, :], 0)
         for part, scales in enumerate((wer_scales, wei_scales)):
             nc.gpsimd.dma_start(out=we_s_raw[ROW0:, part, :], in_=scales.rearrange("a q r -> (a q) r").bitcast(I32))
         nc.gpsimd.dma_start(out=bias_raw[:], in_=b.rearrange("(p h) -> p h", h=2))
 
         nc.sync.dma_start(idx2[:], offs2)
         nc.sync.dma_start(out=tab2_s[ROW1:, :], in_=tab2_scales[0].bitcast(I32))
+        tab2_rows = tab2_words[0].rearrange("p t i -> p (t i)").bitcast(I32)
+        nc.sync.dma_start(out=tab2_w[:, 0 : T // 4], in_=tab2_rows[:, 0 : T // 4])
         nc.sync.dma_start(idx[:], offs)
         nc.sync.dma_start(out=tab_s[ROW0:, :], in_=tab_scales.rearrange("a q t -> (a q) t").bitcast(I32))
         for part, scales in enumerate((wrr_scales, wri_scales)):
             nc.scalar.dma_start(out=wr_s_raw[ROW1:, part, :], in_=scales[0].bitcast(I32))
-        nc.sync.dma_start(out=tab2_w[:], in_=tab2_words[0].rearrange("p t i -> p (t i)").bitcast(I32))
+        nc.sync.dma_start(out=tab2_w[:, T // 4 :], in_=tab2_rows[:, T // 4 :])
         for part, words in enumerate((wrr_words, wri_words)):
             nc.sync.dma_start(out=wr_raw[:, part, :], in_=words[0].bitcast(I32))
         we_raw = []
@@ -81,40 +78,40 @@ def tile_list_ckg_bias_kernel(
             nc.sync.dma_start(out=w_raw[:], in_=words.rearrange("a p r i -> p a (r i)").bitcast(I32))
             we_raw.append(w_raw)
 
-        load_entity_weight(wer_words, keep.tile([P, 2, R], I32, name="wer_raw", align_bytes=64))
         nc.scalar.activation(out=bias[:], in_=bias_raw[:], func=IDENTITY)
 
-        def gather_scales(table_s, offsets, tag):
-            got = raw.tile([P, 16 * offsets.shape[1]], U8, name="got_s", tag=tag, align_bytes=64)
+        def gather_scales(table_s, offsets, got):
             nc.vector.tensor_copy(got[:], table_s[:].bitcast(U8).indirect(offsets))
             return got
 
-        def stage_scales(name, gots, w_s_raws):
+        def stage_scales(name, gots, w_s_raws, row0):
             staged = raw.tile([P, PLANE // 4], I32, name="staged_" + name, tag="then_staged_" + name, align_bytes=64)
             at = 0
             for got in gots:
                 width = got.shape[1] // 4
-                nc.vector.tensor_copy(out=staged[ROW0:, at : at + width], in_=got[ROW0:, :].bitcast(I32))
+                nc.vector.tensor_copy(out=staged[row0:, at : at + width], in_=got[row0:, :].bitcast(I32))
                 at = at + width
             for w_s_raw in w_s_raws:
                 width = w_s_raw.shape[1] * R // 4
                 nc.vector.tensor_copy(
-                    out=staged[ROW0:, at : at + width].rearrange("p (m t g w) -> p m t g w", t=PACK, g=16, w=2),
-                    in_=w_s_raw[ROW0:, :, :].rearrange("p m (g t w) -> p m t g w", t=PACK, w=2),
+                    out=staged[row0:, at : at + width].rearrange("p (m t g w) -> p m t g w", t=PACK, g=16, w=2),
+                    in_=w_s_raw[row0:, :, :].rearrange("p m (g t w) -> p m t g w", t=PACK, w=2),
                 )
                 at = at + width
             return staged
 
-        staged_r = stage_scales("r", [gather_scales(tab2_s, idx2[:], "then_first")], [wr_s_raw])
+        plane_r = stage_scales("r", [gather_scales(tab2_s, idx2[:], laid.tile([P, J], U8, name="got_r", offset=63 * R, align_bytes=64))], [wr_s_raw], 0)
         for r in range(4):
-            nc.sync.dma_start(out=plane_r[r:P:32, :], in_=staged_r[ROW1 + r : P : 4, :])
-        tab_w = raw.tile([P, T], I32, name="tab_w", tag="then_tab", align_bytes=64)
+            nc.sync.dma_start(out=plane_r[r:P:32, :], in_=plane_r[ROW1 + r : P : 4, :])
+        tab_w = laid.tile([P, T], I32, name="tab_w", offset=24 * R, align_bytes=64)
         nc.sync.dma_start(out=tab_w[:], in_=tab_words[0].rearrange("p t i -> p (t i)").bitcast(I32))
+        load_entity_weight(wer_words, laid.tile([P, 2, R], I32, name="wer_raw", offset=16 * R, align_bytes=64))
         halves = [
             (slice(half * HALF, (half + 1) * HALF), slice(half * HALF // 16, (half + 1) * HALF // 16))
             for half in range(2)
         ]
-        got_s = [gather_scales(tab_s, idx[:, halves[0][1]], "then_first")]
+        got_s = [gather_scales(tab_s, idx[:, halves[0][1]], laid.tile([P, HALF], U8, name="got_s0", offset=64 * R, align_bytes=64))]
+        nc.vector.memset(plane_e[:], 0)
         got2_w = []
 
         def gather_relation_words(half, tag):
@@ -128,14 +125,16 @@ def tile_list_ckg_bias_kernel(
             out=wr[:].rearrange("p m (t g w) -> p m t g w", t=PACK, w=4),
             in_=wr_raw[:].rearrange("p m (g t w) -> p m t g w", t=PACK, w=4),
         )
-        got_s.append(gather_scales(tab_s, idx[:, halves[1][1]], "then_second"))
-        staged_e = stage_scales("e", got_s, [we_s_raw])
+        got_s.append(gather_scales(tab_s, idx[:, halves[1][1]], raw.tile([P, HALF], U8, name="got_s1", tag="then_second", align_bytes=64)))
+        staged_e = stage_scales("e", got_s, [we_s_raw], ROW0)
         for a in range(2):
             for r in range(4):
                 first = ROW0 + 16 * a
                 nc.sync.dma_start(out=plane_e[r:P:32, a, :], in_=staged_e[first + r : first + 16 : 4, :])
         load_entity_weight(wei_words, laid.tile([P, 2, R], I32, name="wei_raw", offset=4 * R, align_bytes=64))
         gather_relation_words(1, "then_second")
+        identity = laid.tile([P, P], F32, name="identity", offset=64 * R, align_bytes=64)
+        make_identity(nc, identity[:])
 
         scales_r = plane_r[:].bitcast(U8)
 
@@ -197,26 +196,28 @@ def tile_list_ckg_bias_kernel(
                 in_=we_raw[part][:].rearrange("p a (g t q) -> p a t g q", t=PACK, q=8),
             )
 
-        order_weights(0, nc.vector, "we0")
         got_w = raw.tile([P, J], U32, name="got_w", tag="then_we1", align_bytes=64)
-        parted = [keep.tile([P, 2, 2 * HALF], U8, name="parted%d" % half, align_bytes=64) for half in range(2)]
         for half, (cols, entries) in enumerate(halves):
             nc.vector.tensor_copy(got_w[:, cols], tab_w[:].bitcast(U32).indirect(idx[:, entries]))
+        order_weights(0, nc.vector, "we0")
+        parted = []
+        for first, count in ((0, 2), (2, TILES - 2)):
+            words = laid.tile([P, 2, 2 * count * JT], U8, name="parted%d" % first, offset=16 * R + 4 * first * JT, align_bytes=64)
             nc.vector.tensor_copy(
-                out=parted[half][:].bitcast(U16),
-                in_=got_w[:, cols].bitcast(U16).rearrange("p (j d) -> p d j", d=2),
+                out=words[:].bitcast(U16),
+                in_=got_w[:, first * JT : (first + count) * JT].bitcast(U16).rearrange("p (j d) -> p d j", d=2),
             )
+            parted.extend(words[:, :, 2 * k * JT : 2 * (k + 1) * JT] for k in range(count))
         order_weights(1, nc.vector, "then_we1")
-        n_raw = raw.tile([P, 2, PACK, N], F32, name="n_raw", tag="then_tab", align_bytes=64)
+        n_raw = laid.tile([P, 2, PACK, N], F32, name="n_raw", offset=24 * R, align_bytes=64)
         for part, mat in enumerate((nr, ni)):
             for t in range(PACK):
                 nc.sync.dma_start(out=n_raw[:, part, t, :], in_=mat.rearrange("(g t q) n -> t g q n", t=PACK, q=8)[t])
 
         def entity(i, part):
-            half, at = divmod(i * JT, HALF)
             acc = psum.tile([P, R], F32, name="acc_e", tag="acc_e", bufs=3)
             w_at = J + part * R
-            picked = [parted[half][:, a, 2 * at : 2 * (at + JT)].bitcast(FP4X4) for a in range(2)]
+            picked = [parted[i][:, a, :].bitcast(FP4X4) for a in range(2)]
             scales_e = [plane_e[:, a, :].bitcast(U8) for a in range(2)]
             if i in TURNED:
                 for a in range(2):
@@ -296,7 +297,7 @@ def tile_list_ckg_bias_kernel(
             width = h_mx[0][0].shape[1]
             y = keep.tile([P, 2, width], F32, name="y%d" % first)
             for nh in range(2):
-                tag, bufs = ("acc_e", 3) if first == TILES - 1 else ("acc_y", 2)
+                tag, bufs = ("acc_e", 3) if first == TILES - 1 or (first >= 2 and nh == 1) else ("acc_y", 2)
                 acc = psum.tile([P, width], F32, name="acc_y", tag=tag, bufs=bufs)
                 for part in range(2):
                     n_cols = slice(part * N + nh * P, part * N + (nh + 1) * P)
@@ -309,7 +310,7 @@ def tile_list_ckg_bias_kernel(
                         start=(part == 0),
                         stop=(part == 1),
                     )
-                if first == TILES - 1 and nh == 1:
+                if first >= 6 and nh == 1:
                     nc.vector.tensor_scalar_add(out=y[:, nh, :], in0=acc[:], scalar1=bias[:, nh : nh + 1])
                 else:
                     nc.scalar.activation(out=y[:, nh, :], in_=acc[:], func=IDENTITY, bias=bias[:, nh : nh + 1])
@@ -375,9 +376,7 @@ def tile_list_ckg_bias_kernel(
                     )
             if i == 4:
                 n_mx = quantise("n", n_flat[:])
-            if i == 5:
-                scores(0, n_mx, quantise_h(0))
             if i == 6:
-                scores(2, n_mx, quantise_h(2))
-        for first in (4, last - 1, last):
+                scores(0, n_mx, quantise_h(0))
+        for first in (2, 4, last - 1, last):
             scores(first, n_mx, quantise_h(first))

@@ -26,7 +26,7 @@ HALF = J // 2
 TILES_PER_HALF = HALF // JT
 ROW0, ROW1 = 96, 112
 AHEAD = 5
-TURNED = (3, 7)
+TURNED = (3, 5, 7)
 PLANE = J + 2 * R
 
 
@@ -46,10 +46,10 @@ def tile_list_ckg_bias_kernel(
         idx2 = keep.tile([P, J // 16], U16, name="idx2")
         tab_s = raw.tile([P, T // 4], I32, name="tab_s", tag="then_staged_e", align_bytes=64)
         tab2_s = raw.tile([P, T // 4], I32, name="tab2_s", tag="then_staged_r", align_bytes=64)
-        tab2_w = keep.tile([P, T], I32, name="tab2_w", align_bytes=64)
+        tab2_w = laid.tile([P, T], I32, name="tab2_w", offset=66 * R, align_bytes=64)
         wr_raw = raw.tile([P, 2, R // 2], I32, name="wr_raw", tag="then_second", align_bytes=64)
-        wr_s_raw = laid.tile([P, 2, R // 4], I32, name="wr_s_raw", offset=23 * R, align_bytes=64)
-        we_s_raw = laid.tile([P, 2, R // 4], I32, name="we_s_raw", offset=4 * R, align_bytes=64)
+        wr_s_raw = laid.tile([P, 2, R // 4], I32, name="wr_s_raw", offset=24 * R, align_bytes=64)
+        we_s_raw = laid.tile([P, 2, R // 4], I32, name="we_s_raw", offset=11 * R, align_bytes=64)
         plane_e = laid.tile([P, 2, PLANE // 4], I32, name="plane_e", offset=56 * R, align_bytes=64)
         bias_raw = keep.tile([P, 2], F32, name="bias_raw")
         bias = keep.tile([P, 2], F32, name="bias")
@@ -105,7 +105,6 @@ def tile_list_ckg_bias_kernel(
             nc.sync.dma_start(out=plane_r[r:P:32, :], in_=plane_r[ROW1 + r : P : 4, :])
         tab_w = laid.tile([P, T], I32, name="tab_w", offset=24 * R, align_bytes=64)
         nc.sync.dma_start(out=tab_w[:], in_=tab_words[0].rearrange("p t i -> p (t i)").bitcast(I32))
-        load_entity_weight(wer_words, laid.tile([P, 2, R], I32, name="wer_raw", offset=16 * R, align_bytes=64))
         halves = [
             (slice(half * HALF, (half + 1) * HALF), slice(half * HALF // 16, (half + 1) * HALF // 16))
             for half in range(2)
@@ -131,9 +130,11 @@ def tile_list_ckg_bias_kernel(
             for r in range(4):
                 first = ROW0 + 16 * a
                 nc.sync.dma_start(out=plane_e[r:P:32, a, :], in_=staged_e[first + r : first + 16 : 4, :])
+                if (a, r) == (0, 1):
+                    load_entity_weight(wer_words, laid.tile([P, 2, R], I32, name="wer_raw", offset=12 * R, align_bytes=64))
         load_entity_weight(wei_words, laid.tile([P, 2, R], I32, name="wei_raw", offset=4 * R, align_bytes=64))
         gather_relation_words(1, "then_second")
-        identity = laid.tile([P, P], F32, name="identity", offset=64 * R, align_bytes=64)
+        identity = laid.tile([P, P], F32, name="identity", offset=66 * R, align_bytes=64)
         make_identity(nc, identity[:])
 
         scales_r = plane_r[:].bitcast(U8)
@@ -295,9 +296,12 @@ def tile_list_ckg_bias_kernel(
 
         def scores(first, n_mx, h_mx):
             width = h_mx[0][0].shape[1]
-            y = keep.tile([P, 2, width], F32, name="y%d" % first)
+            if first == 4:
+                y = laid.tile([P, 2, width], F32, name="y%d" % first, offset=2 * R * (first - 2), align_bytes=64)
+            else:
+                y = keep.tile([P, 2, width], F32, name="y%d" % first)
             for nh in range(2):
-                tag, bufs = ("acc_e", 3) if first == TILES - 1 or (first >= 2 and nh == 1) else ("acc_y", 2)
+                tag, bufs = ("acc_y", 2) if first < 4 else ("acc_e", 3) if 2 * first + nh < 13 else ("acc_r", 3)
                 acc = psum.tile([P, width], F32, name="acc_y", tag=tag, bufs=bufs)
                 for part in range(2):
                     n_cols = slice(part * N + nh * P, part * N + (nh + 1) * P)
@@ -310,7 +314,7 @@ def tile_list_ckg_bias_kernel(
                         start=(part == 0),
                         stop=(part == 1),
                     )
-                if first >= 6 and nh == 1:
+                if first >= 2 and nh == 1:
                     nc.vector.tensor_scalar_add(out=y[:, nh, :], in0=acc[:], scalar1=bias[:, nh : nh + 1])
                 else:
                     nc.scalar.activation(out=y[:, nh, :], in_=acc[:], func=IDENTITY, bias=bias[:, nh : nh + 1])
@@ -344,31 +348,50 @@ def tile_list_ckg_bias_kernel(
                 )
             else:
                 product(i, early[i], rels[i], aer, 0)
+        held = {}
         for i in range(TILES):
             with_re = early[i] if i < 2 else work.tile([P, 2, R], F32, name="with_re", tag="with_re")
-            with_im = work.tile([P, 2, R], F32, name="with_im", tag="with_im")
+            if i == last:
+                with_im = laid.tile([P, 2, R], F32, name="last_with_im", offset=0, align_bytes=64)
+            else:
+                with_im = work.tile([P, 2, R], F32, name="with_im", tag="with_im")
             prods = (with_re, with_im)
             if i >= 2:
                 aer = entity(i, 0)
             aei = entity(i, 1)
-            if i >= 2:
+            if i == 6:
+                aer_half = keep.tile([P, R // 2], F32, name="aer_half")
+                nc.scalar.copy(out=aer_half[:].rearrange("p (j t) -> p j t", t=PACK), in_=aer[:, 0 : JT // 2, :])
+                nc.gpsimd.tensor_tensor(
+                    out=with_re[:, :, 0 : R // 2],
+                    in0=rels[i][:, 1:3, 0 : R // 2],
+                    in1=aer_half[:].unsqueeze(1).to_broadcast([P, 2, R // 2]),
+                    op=MULT,
+                )
+                nc.vector.tensor_tensor(
+                    out=like_sums(with_re[:], i)[:, :, JT // 2 :],
+                    in0=like_sums(rels[i][:], i)[:, 1:3, JT // 2 :],
+                    in1=aer[:, JT // 2 :, :].unsqueeze(1).to_broadcast([P, 2, JT // 2, PACK]),
+                    op=MULT,
+                )
+            elif i >= 2:
                 product(i, with_re, rels[i], aer, 0)
+            if i - 2 in TURNED:
+                for part in range(2):
+                    turned_sum(held[i - 2], h_values[i - 2 - i % 2], i % 2, part)
             for terms in (real, imag) if i == last else (slice(0, 2),):
                 product(i, with_im, rels[i], aei, 1, terms)
             if i == last:
                 for part in range(2):
                     turned_sum(prods, h_values[i], 0, part)
             elif i in TURNED:
-                held = prods
+                held[i] = prods
             else:
                 complex_sum(nc.gpsimd, prods, h_values[i - i % 2], i % 2 if i < last - 1 else 0)
             if i + 2 < TILES:
                 negate(rels[i + 2])
             if i + AHEAD < TILES:
                 rels.append(relation(i + AHEAD))
-            if i - 2 in TURNED:
-                for part in range(2):
-                    turned_sum(held, h_values[i - 2 - i % 2], i % 2, part)
             if i == 1:
                 for part in range(2):
                     nc.scalar.copy(

from contextlib import ExitStack

import concourse.mybir as mybir
from concourse.masks import make_identity

K, L, R, N, T, J = 1024, 512, 512, 256, 4096, 1024
FLOPS = 2 * J * (2 * K * R + 2 * L * R + 2 * R * N)

F32 = mybir.dt.float32
BF16 = mybir.dt.bfloat16
I32 = mybir.dt.int32
U32 = mybir.dt.uint32
U16 = mybir.dt.uint16
U8 = mybir.dt.uint8
FP8X4 = mybir.dt.float8_e4m3fn_x4
FP4X4 = mybir.dt.float4_e2m1fn_x4
MULT = mybir.AluOpType.mult
ADD = mybir.AluOpType.add
IDENTITY = mybir.ActivationFunctionType.Identity

P = 128
PACK = 4
JT = 128
TILES = J // JT
HALF = J // 2
TILES_PER_HALF = HALF // JT
ROW0, ROW1 = 96, 112
AHEAD = 5
TURNED = (3, 5, 7)
PLANE = J + 2 * R


def tile_list_ckg_bias_kernel(
    tc, tab_words, tab_scales, tab2_words, tab2_scales, wer_words, wer_scales, wei_words, wei_scales,
    wrr_words, wrr_scales, wri_words, wri_scales, nr, ni, b, offs, offs2, out,
):
    nc = tc.nc
    with ExitStack() as ctx:
        keep = ctx.enter_context(tc.tile_pool(name="keep", bufs=1))
        raw = ctx.enter_context(tc.tile_pool(name="raw", bufs=1))
        laid = ctx.enter_context(tc.tile_pool(name="laid", bufs=1))
        work = ctx.enter_context(tc.tile_pool(name="work", bufs=5))
        psum = ctx.enter_context(tc.psum_pool(name="psum", bufs=2))

        idx = keep.tile([P, J // 16], U16, name="idx")
        idx2 = keep.tile([P, J // 16], U16, name="idx2")
        tab_s = raw.tile([P, T // 4], I32, name="tab_s", tag="then_staged_e", align_bytes=64)
        tab2_s = raw.tile([P, T // 4], I32, name="tab2_s", tag="then_staged_r", align_bytes=64)
        tab2_w = laid.tile([P, T], I32, name="tab2_w", offset=66 * R, align_bytes=64)
        wr_raw = raw.tile([P, 2, R // 2], I32, name="wr_raw", tag="then_second", align_bytes=64)
        wr_s_raw = laid.tile([P, 2, R // 4], I32, name="wr_s_raw", offset=24 * R, align_bytes=64)
        we_s_raw = laid.tile([P, 2, R // 4], I32, name="we_s_raw", offset=11 * R, align_bytes=64)
        plane_e = laid.tile([P, 2, PLANE // 4], I32, name="plane_e", offset=56 * R, align_bytes=64)
        bias_raw = keep.tile([P, 2], F32, name="bias_raw")
        bias = keep.tile([P, 2], F32, name="bias")

        nc.vector.memset(tab2_s[0:ROW1, :], 0)
        nc.vector.memset(wr_s_raw[0:ROW1, :, :], 0)
        nc.gpsimd.memset(tab_s[0:ROW0, :], 0)
        for part, scales in enumerate((wer_scales, wei_scales)):
            nc.gpsimd.dma_start(out=we_s_raw[ROW0:, part, :], in_=scales.rearrange("a q r -> (a q) r").bitcast(I32))
        nc.gpsimd.dma_start(out=bias_raw[:], in_=b.rearrange("(p h) -> p h", h=2))

        nc.sync.dma_start(idx2[:], offs2)
        nc.sync.dma_start(out=tab2_s[ROW1:, :], in_=tab2_scales[0].bitcast(I32))
        tab2_rows = tab2_words[0].rearrange("p t i -> p (t i)").bitcast(I32)
        nc.sync.dma_start(out=tab2_w[:, 0 : T // 4], in_=tab2_rows[:, 0 : T // 4])
        nc.sync.dma_start(idx[:], offs)
        nc.sync.dma_start(out=tab_s[ROW0:, :], in_=tab_scales.rearrange("a q t -> (a q) t").bitcast(I32))
        for part, scales in enumerate((wrr_scales, wri_scales)):
            nc.scalar.dma_start(out=wr_s_raw[ROW1:, part, :], in_=scales[0].bitcast(I32))
        nc.sync.dma_start(out=tab2_w[:, T // 4 :], in_=tab2_rows[:, T // 4 :])
        for part, words in enumerate((wrr_words, wri_words)):
            nc.sync.dma_start(out=wr_raw[:, part, :], in_=words[0].bitcast(I32))
        we_raw = []

        def load_entity_weight(words, w_raw):
            nc.sync.dma_start(out=w_raw[:], in_=words.rearrange("a p r i -> p a (r i)").bitcast(I32))
            we_raw.append(w_raw)

        nc.scalar.activation(out=bias[:], in_=bias_raw[:], func=IDENTITY)

        def gather_scales(table_s, offsets, got):
            nc.vector.tensor_copy(got[:], table_s[:].bitcast(U8).indirect(offsets))
            return got

        def stage_scales(name, gots, w_s_raws, row0):
            staged = raw.tile([P, PLANE // 4], I32, name="staged_" + name, tag="then_staged_" + name, align_bytes=64)
            at = 0
            for got in gots:
                width = got.shape[1] // 4
                nc.vector.tensor_copy(out=staged[row0:, at : at + width], in_=got[row0:, :].bitcast(I32))
                at = at + width
            for w_s_raw in w_s_raws:
                width = w_s_raw.shape[1] * R // 4
                nc.vector.tensor_copy(
                    out=staged[row0:, at : at + width].rearrange("p (m t g w) -> p m t g w", t=PACK, g=16, w=2),
                    in_=w_s_raw[row0:, :, :].rearrange("p m (g t w) -> p m t g w", t=PACK, w=2),
                )
                at = at + width
            return staged

        plane_r = stage_scales("r", [gather_scales(tab2_s, idx2[:], laid.tile([P, J], U8, name="got_r", offset=63 * R, align_bytes=64))], [wr_s_raw], 0)
        for r in range(4):
            nc.sync.dma_start(out=plane_r[r:P:32, :], in_=plane_r[ROW1 + r : P : 4, :])
        tab_w = laid.tile([P, T], I32, name="tab_w", offset=24 * R, align_bytes=64)
        nc.sync.dma_start(out=tab_w[:], in_=tab_words[0].rearrange("p t i -> p (t i)").bitcast(I32))
        halves = [
            (slice(half * HALF, (half + 1) * HALF), slice(half * HALF // 16, (half + 1) * HALF // 16))
            for half in range(2)
        ]
        got_s = [gather_scales(tab_s, idx[:, halves[0][1]], laid.tile([P, HALF], U8, name="got_s0", offset=64 * R, align_bytes=64))]
        nc.vector.memset(plane_e[:], 0)
        got2_w = []

        def gather_relation_words(half, tag):
            got = raw.tile([P, HALF], U32, name="got2_w", tag=tag, align_bytes=64)
            nc.vector.tensor_copy(got[:], tab2_w[:].bitcast(U32).indirect(idx2[:, halves[half][1]]))
            got2_w.append(got)

        gather_relation_words(0, "got2_first")
        wr = keep.tile([P, 2, R // 2], I32, name="wr", align_bytes=64)
        nc.vector.tensor_copy(
            out=wr[:].rearrange("p m (t g w) -> p m t g w", t=PACK, w=4),
            in_=wr_raw[:].rearrange("p m (g t w) -> p m t g w", t=PACK, w=4),
        )
        got_s.append(gather_scales(tab_s, idx[:, halves[1][1]], raw.tile([P, HALF], U8, name="got_s1", tag="then_second", align_bytes=64)))
        staged_e = stage_scales("e", got_s, [we_s_raw], ROW0)
        for a in range(2):
            for r in range(4):
                first = ROW0 + 16 * a
                nc.sync.dma_start(out=plane_e[r:P:32, a, :], in_=staged_e[first + r : first + 16 : 4, :])
                if (a, r) == (0, 1):
                    load_entity_weight(wer_words, laid.tile([P, 2, R], I32, name="wer_raw", offset=12 * R, align_bytes=64))
        load_entity_weight(wei_words, laid.tile([P, 2, R], I32, name="wei_raw", offset=4 * R, align_bytes=64))
        gather_relation_words(1, "then_second")
        identity = laid.tile([P, P], F32, name="identity", offset=66 * R, align_bytes=64)
        make_identity(nc, identity[:])

        scales_r = plane_r[:].bitcast(U8)

        def lanes_last(acc, i):
            if i in TURNED:
                return acc[:]
            return acc[:].rearrange("p (t j) -> p j t", t=PACK)

        def like_sums(values, i):
            if i in TURNED:
                return values
            return values.rearrange("p m (j t) -> p m j t", t=PACK)

        def relation(i):
            half, at = divmod(i * JT, HALF)
            rel = work.tile([P, 3, R], F32, name="rel", tag="rel", bufs=AHEAD)
            picked = got2_w[half][:, at : at + JT].bitcast(FP8X4)
            picked_scale = scales_r[:, i * JT : (i + 1) * JT]
            for part in range(2):
                acc = psum.tile([P, R], F32, name="acc_r", tag="acc_r", bufs=3)
                w_at = J + part * R
                if i in TURNED:
                    nc.tensor.matmul_mx(
                        out=acc[:],
                        lhsT=picked,
                        lhsT_scale=picked_scale,
                        rhs=wr[:, part, :].bitcast(FP4X4),
                        rhs_scale=scales_r[:, w_at : w_at + R],
                        start=True,
                        stop=True,
                    )
                else:
                    for t in range(PACK):
                        nc.tensor.matmul_mx(
                            out=acc[:, t * JT : (t + 1) * JT],
                            lhsT=wr[:, part, t * P // 2 : (t + 1) * P // 2].bitcast(FP4X4),
                            lhsT_scale=scales_r[:, w_at + t * P : w_at + (t + 1) * P],
                            rhs=picked,
                            rhs_scale=picked_scale,
                            start=True,
                            stop=True,
                        )
                nc.scalar.copy(out=like_sums(rel[:], i)[:, 1 + part], in_=lanes_last(acc, i))
            return rel

        def negate(rel):
            nc.scalar.mul(out=rel[:, 0, :], in_=rel[:, 2, :], mul=-1.0)

        rels = [relation(i) for i in range(AHEAD)]
        for rel in rels[:2]:
            negate(rel)

        we = []

        def order_weights(part, engine, tag):
            we.append(raw.tile([P, 2, R], I32, name="we", tag=tag, align_bytes=64))
            engine.tensor_copy(
                out=we[part][:].rearrange("p a (t g q) -> p a t g q", t=PACK, q=8),
                in_=we_raw[part][:].rearrange("p a (g t q) -> p a t g q", t=PACK, q=8),
            )

        got_w = raw.tile([P, J], U32, name="got_w", tag="then_we1", align_bytes=64)
        for half, (cols, entries) in enumerate(halves):
            nc.vector.tensor_copy(got_w[:, cols], tab_w[:].bitcast(U32).indirect(idx[:, entries]))
        order_weights(0, nc.vector, "we0")
        parted = []
        for first, count in ((0, 2), (2, TILES - 2)):
            words = laid.tile([P, 2, 2 * count * JT], U8, name="parted%d" % first, offset=16 * R + 4 * first * JT, align_bytes=64)
            nc.vector.tensor_copy(
                out=words[:].bitcast(U16),
                in_=got_w[:, first * JT : (first + count) * JT].bitcast(U16).rearrange("p (j d) -> p d j", d=2),
            )
            parted.extend(words[:, :, 2 * k * JT : 2 * (k + 1) * JT] for k in range(count))
        order_weights(1, nc.vector, "then_we1")
        n_raw = laid.tile([P, 2, PACK, N], F32, name="n_raw", offset=24 * R, align_bytes=64)
        for part, mat in enumerate((nr, ni)):
            for t in range(PACK):
                nc.sync.dma_start(out=n_raw[:, part, t, :], in_=mat.rearrange("(g t q) n -> t g q n", t=PACK, q=8)[t])

        def entity(i, part):
            acc = psum.tile([P, R], F32, name="acc_e", tag="acc_e", bufs=3)
            w_at = J + part * R
            picked = [parted[i][:, a, :].bitcast(FP4X4) for a in range(2)]
            scales_e = [plane_e[:, a, :].bitcast(U8) for a in range(2)]
            if i in TURNED:
                for a in range(2):
                    nc.tensor.matmul_mx(
                        out=acc[:],
                        lhsT=picked[a],
                        lhsT_scale=scales_e[a][:, i * JT : (i + 1) * JT],
                        rhs=we[part][:, a, :].bitcast(FP8X4),
                        rhs_scale=scales_e[a][:, w_at : w_at + R],
                        start=(a == 0),
                        stop=(a == 1),
                    )
            else:
                for t in range(PACK):
                    for a in range(2):
                        nc.tensor.matmul_mx(
                            out=acc[:, t * JT : (t + 1) * JT],
                            lhsT=we[part][:, a, t * P : (t + 1) * P].bitcast(FP8X4),
                            lhsT_scale=scales_e[a][:, w_at + t * P : w_at + (t + 1) * P],
                            rhs=picked[a],
                            rhs_scale=scales_e[a][:, i * JT : (i + 1) * JT],
                            start=(a == 0),
                            stop=(a == 1),
                        )
            return lanes_last(acc, i)

        def product(i, prod, rel, acc, part, terms=slice(0, 2)):
            count = terms.stop - terms.start
            at = 1 - part + terms.start
            nc.vector.tensor_tensor(
                out=like_sums(prod[:], i)[:, terms],
                in0=like_sums(rel[:], i)[:, at : at + count],
                in1=acc.unsqueeze(1).to_broadcast([P, count] + list(acc.shape[1:])),
                op=MULT,
            )

        def complex_sum(adder, prods, h, slot, parts=slice(0, 2)):
            h_view = h.rearrange("p (m i c) -> p m i c", m=2, c=JT * PACK)
            adder.tensor_tensor(out=h_view[:, parts, slot, :], in0=prods[0][:, parts, :], in1=prods[1][:, parts, :], op=ADD)

        def turned_sum(prods, h, slot, part):
            acc = psum.tile([P, PACK, JT], F32, name="acc_h", tag="acc_r", bufs=3)
            for term, prod in enumerate(prods):
                for t in range(PACK):
                    nc.tensor.matmul(
                        out=acc[:, t, :],
                        lhsT=prod[:, part, t * P : (t + 1) * P],
                        rhs=identity[:],
                        is_transpose=True,
                        start=(term == 0 and t == 0),
                        stop=(term == 1 and t == PACK - 1),
                    )
            nc.scalar.copy(
                out=h.rearrange("p (m i j t) -> p m i j t", m=2, j=JT, t=PACK)[:, part, slot],
                in_=acc[:].rearrange("p t j -> p j t"),
            )

        def quantise(name, values):
            width = values.shape[1] // PACK
            codes = keep.tile([P, width], U32, name=name + "_codes", align_bytes=64)
            scales = keep.tile([P, width], U8, name=name + "_scales", align_bytes=64)
            nc.vector.quantize_mx(out=codes[:].bitcast(FP8X4), scales=scales[:], in_=values)
            return codes[:], scales[:]

        out_rows = out.rearrange("(p h) j -> p h j", h=2)

        def quantise_h(first):
            values = h_values[first]
            width = values.shape[1] // 2
            if first == TILES - 1:
                return [quantise("h%d_%d" % (first, part), values[:, part * width : (part + 1) * width]) for part in range(2)]
            codes, scales = quantise("h%d" % first, values)
            words = width // PACK
            return [(codes[:, part * words : (part + 1) * words], scales[:, part * words : (part + 1) * words]) for part in range(2)]

        def scores(first, n_mx, h_mx):
            width = h_mx[0][0].shape[1]
            if first == 4:
                y = laid.tile([P, 2, width], F32, name="y%d" % first, offset=2 * R * (first - 2), align_bytes=64)
            else:
                y = keep.tile([P, 2, width], F32, name="y%d" % first)
            for nh in range(2):
                tag, bufs = ("acc_y", 2) if first < 4 else ("acc_e", 3) if 2 * first + nh < 13 else ("acc_r", 3)
                acc = psum.tile([P, width], F32, name="acc_y", tag=tag, bufs=bufs)
                for part in range(2):
                    n_cols = slice(part * N + nh * P, part * N + (nh + 1) * P)
                    nc.tensor.matmul_mx(
                        out=acc[:],
                        lhsT=n_mx[0][:, n_cols].bitcast(FP8X4),
                        lhsT_scale=n_mx[1][:, n_cols],
                        rhs=h_mx[part][0].bitcast(FP8X4),
                        rhs_scale=h_mx[part][1],
                        start=(part == 0),
                        stop=(part == 1),
                    )
                if first >= 2 and nh == 1:
                    nc.vector.tensor_scalar_add(out=y[:, nh, :], in0=acc[:], scalar1=bias[:, nh : nh + 1])
                else:
                    nc.scalar.activation(out=y[:, nh, :], in_=acc[:], func=IDENTITY, bias=bias[:, nh : nh + 1])
            cols = slice(first * JT, first * JT + width)
            if first == TILES - 1:
                for nh, queue in enumerate((nc.scalar, nc.sync)):
                    queue.dma_start(out=out_rows[:, nh, cols], in_=y[:, nh, :])
            else:
                nc.sync.dma_start(out=out_rows[:, :, cols], in_=y[:])

        tile_width = 2 * JT * PACK
        n_flat = keep.tile([P, 2 * N * PACK], BF16, name="n_flat", align_bytes=64)
        n_values = n_flat[:].rearrange("p (a h m t) -> p a h m t", a=2, h=2, t=PACK)
        last = TILES - 1
        h_values = {}
        for first in range(0, last - 1, 2):
            h_values[first] = keep.tile([P, 2 * tile_width], BF16, name="h%d" % first, align_bytes=64)[:]
        for first in (last - 1, last):
            h_values[first] = keep.tile([P, tile_width], BF16, name="h%d" % first, align_bytes=64)[:]

        real, imag = slice(0, 1), slice(1, 2)
        early = []
        for i in range(2):
            aer = entity(i, 0)
            early.append(laid.tile([P, 2, R], F32, name="early%d" % i, offset=8 * R * i, align_bytes=64))
            if i == 0:
                aer_out = keep.tile([P, R], F32, name="aer_out")
                nc.scalar.copy(out=aer_out[:].rearrange("p (j t) -> p j t", t=PACK), in_=aer)
                nc.gpsimd.tensor_tensor(
                    out=early[i][:], in0=rels[i][:, 1:3, :], in1=aer_out[:].unsqueeze(1).to_broadcast([P, 2, R]), op=MULT
                )
            else:
                product(i, early[i], rels[i], aer, 0)
        held = {}
        for i in range(TILES):
            with_re = early[i] if i < 2 else work.tile([P, 2, R], F32, name="with_re", tag="with_re")
            if i == last:
                with_im = laid.tile([P, 2, R], F32, name="last_with_im", offset=0, align_bytes=64)
            else:
                with_im = work.tile([P, 2, R], F32, name="with_im", tag="with_im")
            prods = (with_re, with_im)
            if i >= 2:
                aer = entity(i, 0)
            aei = entity(i, 1)
            if i == 6:
                aer_half = keep.tile([P, R // 2], F32, name="aer_half")
                nc.scalar.copy(out=aer_half[:].rearrange("p (j t) -> p j t", t=PACK), in_=aer[:, 0 : JT // 2, :])
                nc.gpsimd.tensor_tensor(
                    out=with_re[:, :, 0 : R // 2],
                    in0=rels[i][:, 1:3, 0 : R // 2],
                    in1=aer_half[:].unsqueeze(1).to_broadcast([P, 2, R // 2]),
                    op=MULT,
                )
                nc.vector.tensor_tensor(
                    out=like_sums(with_re[:], i)[:, :, JT // 2 :],
                    in0=like_sums(rels[i][:], i)[:, 1:3, JT // 2 :],
                    in1=aer[:, JT // 2 :, :].unsqueeze(1).to_broadcast([P, 2, JT // 2, PACK]),
                    op=MULT,
                )
            elif i >= 2:
                product(i, with_re, rels[i], aer, 0)
            if i - 2 in TURNED:
                for part in range(2):
                    turned_sum(held[i - 2], h_values[i - 2 - i % 2], i % 2, part)
            for terms in (real, imag) if i == last else (slice(0, 2),):
                product(i, with_im, rels[i], aei, 1, terms)
            if i == last:
                for part in range(2):
                    turned_sum(prods, h_values[i], 0, part)
            elif i in TURNED:
                held[i] = prods
            else:
                complex_sum(nc.gpsimd, prods, h_values[i - i % 2], i % 2 if i < last - 1 else 0)
            if i + 2 < TILES:
                negate(rels[i + 2])
            if i + AHEAD < TILES:
                rels.append(relation(i + AHEAD))
            if i == 1:
                for part in range(2):
                    nc.scalar.copy(
                        out=n_values[:, part, :, :, :], in_=n_raw[:, part, :, :].rearrange("p t (m h) -> p h m t", h=2)
                    )
            if i == 4:
                n_mx = quantise("n", n_flat[:])
            if i == 6:
                scores(0, n_mx, quantise_h(0))
        for first in (2, 4, last - 1, last):
            scores(first, n_mx, quantise_h(first))
